import numpy as np
import ml_dtypes


def mxq(x, axis, fmt="e4m3"):
    dtype, down = {"e4m3": (ml_dtypes.float8_e4m3fn, 7), "e5m2": (ml_dtypes.float8_e5m2, 14)}[fmt]
    v = np.moveaxis(np.asarray(x, np.float32).astype(ml_dtypes.bfloat16).astype(np.float64), axis, -1)
    blocks = v.reshape(v.shape[:-1] + (-1, 32))
    amax = np.abs(blocks).max(-1, keepdims=True)
    byte = np.maximum(np.where(amax > 0, np.frexp(amax)[1] - 1 + 127, 0) - down, 1)
    scale = np.exp2(byte - 127.0)
    codes = (blocks / scale).astype(np.float32).astype(dtype).astype(np.float64)
    return np.moveaxis((codes * scale).reshape(v.shape), -1, axis)


WIDE = False


def mx_kscale(k):
    if not WIDE:
        return np.ones(k)
    levels = np.array([10, -10, 5, -5, 0])
    if k % 512:
        return np.exp2(np.random.permutation(np.resize(levels, k // 32))).repeat(32)
    a = np.empty((k // 512, 16))
    for p in range(k // 512):
        a[p, :8] = np.random.permutation(np.resize(levels, 8))
        for g in range(8):
            far = levels[np.abs(levels - a[p, g]) >= 10]
            a[p, g + 8] = far[np.random.randint(len(far))]
    return np.exp2(a.ravel()).repeat(32)


def f64(x):
    return np.asarray(x).astype(np.float64)


def striped(idx):
    return np.tile(idx.reshape(-1, 16).T, (8, 1)).astype(np.uint16)


def unstriped(offs):
    return offs[:16].T.reshape(-1).astype(np.int64)


def striped8(idx):
    return np.concatenate([x.reshape(-1, 16).T for x in idx]).astype(np.uint16)


def runs(offs, k):
    lists = np.stack([offs[16 * r : 16 * r + 16].T.reshape(-1) for r in range(8)]).astype(np.int64)
    return lists[np.arange(k) % 512 // 64]


def pack_weight(w):
    k, n = w.shape
    w = f64(np.asarray(w, np.float32).astype(ml_dtypes.bfloat16)).reshape(k // 32, 32, n)
    amax = np.abs(w).max(1)
    byte = np.clip(np.where(amax > 0, np.frexp(amax)[1] - 1 + 127 - 7, 1), 1, 254)
    scaled = (w * np.exp2(127.0 - byte)[:, None, :]).reshape(k, n).astype(np.float32)
    words = np.ascontiguousarray(scaled.reshape(k // 512, 128, 4, n).transpose(0, 1, 3, 2)).astype(ml_dtypes.float8_e4m3fn).view(np.uint8)
    return words, np.ascontiguousarray(byte.astype(np.uint8).reshape(k // 512, 16, n))


def unpack_weight(words, scales):
    g, p, n, _ = words.shape
    vals = np.ascontiguousarray(words).view(ml_dtypes.float8_e4m3fn).astype(np.float64) * np.repeat(np.exp2(scales.astype(np.float64) - 127.0), 8, axis=1)[..., None]
    return vals.transpose(0, 1, 3, 2).reshape(g * 512, n)


K, T, S, V, N, H = 512, 2048, 512, 256, 512, 512


def setup_inputs():
    n = np.random.standard_normal
    s = mx_kscale(K)[:, None]
    u = mx_kscale(H)
    packed_xT = pack_weight(n((K, T)) * s)
    return {
        "x_words": packed_xT[0],
        "x_scales": packed_xT[1],
        "w1": (n((K, H)) / np.sqrt(K) / s * u).astype(np.float32),
        "w2": (n((H, N)) / np.sqrt(H) / u[:, None]).astype(np.float32),
        "offs": striped(np.random.permutation(T)[:S]),
        "s1": striped8(np.stack([np.random.permutation(S)[:V] for _ in range(8)])),
        "d1": striped8(np.stack([np.random.permutation(S)[:V] for _ in range(8)])),
        "s2": striped8(np.stack([np.random.permutation(S)[:V] for _ in range(8)])),
        "d2": striped8(np.stack([np.random.permutation(S)[:V] for _ in range(8)])),
    }


def reference(x_words, x_scales, w1, w2, offs, s1, d1, s2, d2):
    xq = unpack_weight(x_words, x_scales)[:, unstriped(offs)]
    y = mxq(f64(w1), 0, "e4m3").T @ xq
    m1 = y[np.arange(H)[:, None], runs(s1, H)]
    h = y.copy()
    h[np.arange(H)[:, None], runs(d1, H)] = m1
    m2 = 0.5 * (h[np.arange(H)[:, None], runs(s2, H)] + h[np.arange(H)[:, None], runs(d2, H)])
    z = h.copy()
    z[np.arange(H)[:, None], runs(d2, H)] = m2
    return mxq(f64(w2), 0, "e4m3").T @ mxq(z, 0, "e4m3")

@@ -1,0 +1,164 @@
+from contextlib import ExitStack
+
+import concourse.mybir as mybir
+
+K, T, S, V, H, N = 512, 2048, 512, 256, 512, 512
+FLOPS = 2 * K * H * S + 2 * H * N * S
+
+F32 = mybir.dt.float32
+BF16 = mybir.dt.bfloat16
+I32 = mybir.dt.int32
+U32 = mybir.dt.uint32
+U16 = mybir.dt.uint16
+U8 = mybir.dt.uint8
+FP8X4 = mybir.dt.float8_e4m3fn_x4
+MULT = mybir.AluOpType.mult
+ADD = mybir.AluOpType.add
+
+P = 128
+PACK = 4
+HALF = 256
+ORDER = (0, 1, 3, 2)
+
+
+def tile_picked_carry2_none_p_kernel(tc, x_words, x_scales, w1, w2, offs, s1, d1, s2, d2, out):
+    nc = tc.nc
+    with ExitStack() as ctx:
+        lists = ctx.enter_context(tc.tile_pool(name="lists", bufs=1))
+        keep = ctx.enter_context(tc.tile_pool(name="keep", bufs=1))
+        psum = ctx.enter_context(tc.psum_pool(name="psum", bufs=8))
+
+        def sb(name, shape, dtype):
+            return keep.tile(shape, dtype, name=name, align_bytes=64)
+
+        offs_t = lists.tile([P, S // 16], U16, name="offs_t")
+        s1_t = lists.tile([P, V // 16], U16, name="s1_t")
+        d1_t = lists.tile([P, V // 16], U16, name="d1_t")
+        s2_t = lists.tile([P, V // 16], U16, name="s2_t")
+        d2_t = lists.tile([P, V // 16], U16, name="d2_t")
+
+        xs = sb("xs", [P, T], U8)
+        nc.vector.memset(xs[:].bitcast(I32), 0)
+        xw = sb("xw", [P, T], U32)
+        nc.sync.dma_start(offs_t[:], offs)
+        nc.sync.dma_start(xw[:].bitcast(I32), x_words[0].rearrange("p n t -> p (n t)").bitcast(I32))
+        for q in range(4):
+            nc.sync.dma_start(xs[32 * q : 32 * q + 4, :].bitcast(I32), x_scales[0, 4 * q : 4 * q + 4, :].bitcast(I32))
+        w1_raw = [sb("w1_raw%d" % h, [P, PACK, HALF], F32) for h in range(2)]
+        for h in range(2):
+            nc.sync.dma_start(w1_raw[h][:], w1[:, HALF * h : HALF * (h + 1)].rearrange("(p j) c -> p j c", j=PACK))
+        for tile, src in ((s1_t, s1), (d1_t, d1), (s2_t, s2), (d2_t, d2)):
+            nc.sync.dma_start(tile[:], src)
+        w2_raw = sb("w2_raw", [P, PACK, N], F32)
+        nc.sync.dma_start(w2_raw[:], w2.rearrange("(p j) c -> p j c", j=PACK))
+
+        xg_s = sb("xg_s", [P, S], U8)
+        xg_w = sb("xg_w", [P, S], U32)
+        nc.vector.tensor_copy(xg_s[:], xs[:].indirect(offs_t[:]))
+        nc.vector.tensor_copy(xg_w[:], xw[:].indirect(offs_t[:]))
+
+        MH = P // 2
+        g0 = [sb("w1_g0_%d" % h, [P, MH, PACK], BF16) for h in range(2)]
+        gr = sb("w1_gr", [P, PACK - 1, P, PACK], BF16)
+        c0 = sb("w1_c0", [P, P], U32)
+        e0 = sb("w1_e0", [P, P], U8)
+        cr = [sb("w1_c%d" % t, [P, P], U32) for t in range(1, PACK)]
+        er = [sb("w1_e%d" % t, [P, P], U8) for t in range(1, PACK)]
+
+        def w1_view(h):
+            return w1_raw[h][:].rearrange("p j (m t) -> p m j t", t=PACK)
+
+        def gr_view(h):
+            return gr[:, :, MH * h : MH * (h + 1), :].rearrange("p t m j -> p m j t")
+
+        def quant0(h):
+            nc.vector.quantize_mx(out=c0[:, MH * h : MH * (h + 1)].bitcast(FP8X4), scales=e0[:, MH * h : MH * (h + 1)], in_=g0[h][:].rearrange("p m j -> p (m j)"))
+
+        nc.scalar.copy(g0[0][:], w1_view(0)[:, :, :, 0])
+        nc.scalar.copy(gr_view(0), w1_view(0)[:, :, :, 1:PACK])
+        quant0(0)
+        nc.vector.tensor_copy(g0[1][:], w1_view(1)[:, :, :, 0])
+        quant0(1)
+        nc.vector.tensor_copy(gr_view(1), w1_view(1)[:, :, :, 1:PACK])
+
+        def quant_rest(t):
+            nc.vector.quantize_mx(out=cr[t - 1][:].bitcast(FP8X4), scales=er[t - 1][:], in_=gr[:, t - 1, :, :].rearrange("p m j -> p (m j)"))
+
+        state = [sb("state%d" % t, [P, S], F32) for t in range(PACK)]
+
+        def project(t, codes, scales, pieces):
+            width = S // pieces
+            for c in range(pieces):
+                cols = slice(width * c, width * (c + 1))
+                acc = psum.tile([P, width], F32, name="acc")
+                nc.tensor.matmul_mx(out=acc[:], lhsT=codes[:].bitcast(FP8X4), lhsT_scale=scales[:], rhs=xg_w[:, cols].bitcast(FP8X4), rhs_scale=xg_s[:, cols], start=True, stop=True)
+                nc.scalar.copy(state[t][:, cols], acc[:])
+
+        project(0, c0, e0, 2)
+        for t in ORDER[1:]:
+            quant_rest(t)
+            project(t, cr[t - 1], er[t - 1], 1)
+
+        w2_g = sb("w2_g", [P, N, PACK], BF16)
+        nc.scalar.copy(w2_g[:].rearrange("p (c i) j -> p c j i", i=4), w2_raw[:].rearrange("p j (c i) -> p c j i", i=4))
+        w2_c = sb("w2_c", [P, N], U32)
+        w2_e = sb("w2_e", [P, N], U8)
+
+        m1 = [sb("m1_%d" % t, [P, V], F32) for t in range(PACK)]
+        ms = [sb("ms_%d" % t, [P, V], F32) for t in range(PACK)]
+        md = [sb("md_%d" % t, [P, V], F32) for t in range(PACK)]
+        pair = sb("pair", [P, 2 * S], F32)
+        zb = [sb("zb%d" % c, [P, HALF, PACK], BF16) for c in range(2)]
+
+        def fetch1(t):
+            nc.vector.tensor_copy(m1[t][:], state[t][:].indirect(s1_t[:]))
+
+        def put1(t):
+            nc.vector.tensor_copy(state[t][:].indirect(d1_t[:]), m1[t][:])
+            if t == 2:
+                nc.scalar.copy(pair[:, 0:S], state[t][:])
+
+        def fetch2(t):
+            nc.vector.tensor_scalar(ms[t][:], state[t][:].indirect(s2_t[:]), 0.5, 0.0, op0=MULT, op1=ADD)
+            nc.vector.tensor_scalar(md[t][:], state[t][:].indirect(d2_t[:]), 0.5, 0.0, op0=MULT, op1=ADD)
+
+        def put2(t):
+            window = pair if t == 2 else state[t]
+            nc.vector.tensor_tensor(window[:].indirect(d2_t[:]), ms[t][:], md[t][:], ADD)
+            if t < 2:
+                for c in range(2):
+                    nc.scalar.copy(zb[c][:, :, t], state[t][:, HALF * c : HALF * (c + 1)])
+            if t == 3:
+                nc.scalar.copy(pair[:, S : 2 * S], state[t][:])
+
+        fetch1(ORDER[0])
+        put1(ORDER[0])
+        for i in range(PACK):
+            t = ORDER[i]
+            if i + 1 < PACK:
+                fetch1(ORDER[i + 1])
+            fetch2(t)
+            if i + 1 < PACK:
+                put1(ORDER[i + 1])
+            else:
+                nc.vector.quantize_mx(out=w2_c[:].bitcast(FP8X4), scales=w2_e[:], in_=w2_g[:].rearrange("p c j -> p (c j)"))
+            put2(t)
+
+        pair_v = pair[:].rearrange("p (s j) -> p j s", s=2)
+        z_c = [sb("z_c%d" % c, [P, HALF], U32) for c in range(2)]
+        z_e = [sb("z_e%d" % c, [P, HALF], U8) for c in range(2)]
+        nc.vector.tensor_copy(zb[0][:, :, 2:4], pair_v[:, 0:HALF, :])
+        nc.scalar.copy(zb[1][:, :, 2:4], pair_v[:, HALF:S, :])
+        for c in range(2):
+            nc.vector.quantize_mx(out=z_c[c][:].bitcast(FP8X4), scales=z_e[c][:], in_=zb[c][:].rearrange("p n j -> p (n j)"))
+        for c in range(2):
+            for b in range(PACK):
+                rows = slice(P * b, P * (b + 1))
+                acc = psum.tile([P, HALF], F32, name="acc")
+                nc.tensor.matmul_mx(out=acc[:], lhsT=w2_c[:, rows].bitcast(FP8X4), lhsT_scale=w2_e[:, rows], rhs=z_c[c][:].bitcast(FP8X4), rhs_scale=z_e[c][:], start=True, stop=True)
+                res = sb("res%d_%d" % (c, b), [P, HALF], F32)
+                if b % 2 == 0:
+                    nc.scalar.copy(res[:], acc[:])
+                else:
+                    nc.vector.tensor_copy(res[:], acc[:])
+                nc.sync.dma_start(out[rows, HALF * c : HALF * (c + 1)], res[:])

@@ -19,6 +19,7 @@ P = 128
 PACK = 4
 HALF = 256
 ORDER = (0, 1, 3, 2)
+CHUNKS = ((0, 128), (128, 128), (256, 256))
 
 
 def tile_picked_carry2_none_p_kernel(tc, x_words, x_scales, w1, w2, offs, s1, d1, s2, d2, out):
@@ -28,8 +29,8 @@ def tile_picked_carry2_none_p_kernel(tc, x_words, x_scales, w1, w2, offs, s1, d1
         keep = ctx.enter_context(tc.tile_pool(name="keep", bufs=1))
         psum = ctx.enter_context(tc.psum_pool(name="psum", bufs=8))
 
-        def sb(name, shape, dtype):
-            return keep.tile(shape, dtype, name=name, align_bytes=64)
+        def sb(name, shape, dtype, tag=None):
+            return keep.tile(shape, dtype, name=name, tag=tag or name, align_bytes=64)
 
         offs_t = lists.tile([P, S // 16], U16, name="offs_t")
         s1_t = lists.tile([P, V // 16], U16, name="s1_t")
@@ -40,77 +41,82 @@ def tile_picked_carry2_none_p_kernel(tc, x_words, x_scales, w1, w2, offs, s1, d1
         xs = sb("xs", [P, T], U8)
         nc.vector.memset(xs[:].bitcast(I32), 0)
         xw = sb("xw", [P, T], U32)
-        nc.sync.dma_start(offs_t[:], offs)
-        nc.sync.dma_start(xw[:].bitcast(I32), x_words[0].rearrange("p n t -> p (n t)").bitcast(I32))
-        for q in range(4):
-            nc.sync.dma_start(xs[32 * q : 32 * q + 4, :].bitcast(I32), x_scales[0, 4 * q : 4 * q + 4, :].bitcast(I32))
-        w1_raw = [sb("w1_raw%d" % h, [P, PACK, HALF], F32) for h in range(2)]
-        for h in range(2):
-            nc.sync.dma_start(w1_raw[h][:], w1[:, HALF * h : HALF * (h + 1)].rearrange("(p j) c -> p j c", j=PACK))
-        for tile, src in ((s1_t, s1), (d1_t, d1), (s2_t, s2), (d2_t, d2)):
-            nc.sync.dma_start(tile[:], src)
+        w1_raw = sb("w1_raw", [P, PACK, H], F32)
         w2_raw = sb("w2_raw", [P, PACK, N], F32)
+
+        def ld_sc(eng):
+            for q in range(4):
+                eng.dma_start(xs[32 * q : 32 * q + 4, :].bitcast(I32), x_scales[0, 4 * q : 4 * q + 4, :].bitcast(I32))
+
+        def ld_x():
+            nc.sync.dma_start(xw[:].bitcast(I32), x_words[0].rearrange("p n t -> p (n t)").bitcast(I32))
+
+        nc.sync.dma_start(w1_raw[:], w1.rearrange("(p j) c -> p j c", j=PACK))
+        nc.sync.dma_start(offs_t[:], offs)
+        nc.sync.dma_start(s1_t[:], s1)
+        ld_sc(nc.sync)
+        ld_x()
+        for tile, src in ((d1_t, d1), (s2_t, s2), (d2_t, d2)):
+            nc.sync.dma_start(tile[:], src)
         nc.sync.dma_start(w2_raw[:], w2.rearrange("(p j) c -> p j c", j=PACK))
 
+        w1_g = [sb("w1_g%d" % u, [P, 2, P, PACK], BF16) for u in range(2)]
+        w1_c = [None, None]
+        w1_e = [sb("w1_e%d" % u, [P, 2 * P], U8) for u in range(2)]
+
+        def w1_weave(copy, u):
+            src = w1_raw[:].rearrange("p j (m t) -> p m j t", t=PACK)[:, :, :, 2 * u : 2 * u + 2]
+            copy(w1_g[u][:].rearrange("p t m j -> p m j t"), src)
+
+        def w1_quant(u):
+            w1_c[u] = sb("w1_c%d" % u, [P, 2 * P], U32, tag="xw" if u == 1 else None)
+            nc.vector.quantize_mx(out=w1_c[u][:].bitcast(FP8X4), scales=w1_e[u][:], in_=w1_g[u][:].rearrange("p t m j -> p (t m j)"))
+
         xg_s = sb("xg_s", [P, S], U8)
-        xg_w = sb("xg_w", [P, S], U32)
+        xg_w = [sb("xg_w%d" % c, [P, HALF], U32) for c in range(2)]
+
+        w1_weave(nc.vector.tensor_copy, 0)
+        w1_weave(nc.scalar.copy, 1)
         nc.vector.tensor_copy(xg_s[:], xs[:].indirect(offs_t[:]))
-        nc.vector.tensor_copy(xg_w[:], xw[:].indirect(offs_t[:]))
-
-        MH = P // 2
-        g0 = [sb("w1_g0_%d" % h, [P, MH, PACK], BF16) for h in range(2)]
-        gr = sb("w1_gr", [P, PACK - 1, P, PACK], BF16)
-        c0 = sb("w1_c0", [P, P], U32)
-        e0 = sb("w1_e0", [P, P], U8)
-        cr = [sb("w1_c%d" % t, [P, P], U32) for t in range(1, PACK)]
-        er = [sb("w1_e%d" % t, [P, P], U8) for t in range(1, PACK)]
-
-        def w1_view(h):
-            return w1_raw[h][:].rearrange("p j (m t) -> p m j t", t=PACK)
-
-        def gr_view(h):
-            return gr[:, :, MH * h : MH * (h + 1), :].rearrange("p t m j -> p m j t")
-
-        def quant0(h):
-            nc.vector.quantize_mx(out=c0[:, MH * h : MH * (h + 1)].bitcast(FP8X4), scales=e0[:, MH * h : MH * (h + 1)], in_=g0[h][:].rearrange("p m j -> p (m j)"))
-
-        nc.scalar.copy(g0[0][:], w1_view(0)[:, :, :, 0])
-        nc.scalar.copy(gr_view(0), w1_view(0)[:, :, :, 1:PACK])
-        quant0(0)
-        nc.vector.tensor_copy(g0[1][:], w1_view(1)[:, :, :, 0])
-        quant0(1)
-        nc.vector.tensor_copy(gr_view(1), w1_view(1)[:, :, :, 1:PACK])
-
-        def quant_rest(t):
-            nc.vector.quantize_mx(out=cr[t - 1][:].bitcast(FP8X4), scales=er[t - 1][:], in_=gr[:, t - 1, :, :].rearrange("p m j -> p (m j)"))
+        w1_quant(0)
+        for c in range(2):
+            nc.vector.tensor_copy(xg_w[c][:], xw[:].indirect(offs_t[:, 16 * c : 16 * (c + 1)]))
+        w1_quant(1)
 
         state = [sb("state%d" % t, [P, S], F32) for t in range(PACK)]
 
-        def project(t, codes, scales, pieces):
-            width = S // pieces
-            for c in range(pieces):
-                cols = slice(width * c, width * (c + 1))
-                acc = psum.tile([P, width], F32, name="acc")
-                nc.tensor.matmul_mx(out=acc[:], lhsT=codes[:].bitcast(FP8X4), lhsT_scale=scales[:], rhs=xg_w[:, cols].bitcast(FP8X4), rhs_scale=xg_s[:, cols], start=True, stop=True)
-                nc.scalar.copy(state[t][:, cols], acc[:])
+        def project(t, start, width, copy):
+            cols = slice(start, start + width)
+            c = start // HALF
+            local = slice(start - HALF * c, start - HALF * c + width)
+            feats = slice(P * (t % 2), P * (t % 2 + 1))
+            acc = psum.tile([P, width], F32, name="acc")
+            nc.tensor.matmul_mx(out=acc[:], lhsT=w1_c[t // 2][:, feats].bitcast(FP8X4), lhsT_scale=w1_e[t // 2][:, feats], rhs=xg_w[c][:, local].bitcast(FP8X4), rhs_scale=xg_s[:, cols], start=True, stop=True)
+            copy(state[t][:, cols], acc[:])
 
-        project(0, c0, e0, 2)
-        for t in ORDER[1:]:
-            quant_rest(t)
-            project(t, cr[t - 1], er[t - 1], 1)
+        project(0, 0, HALF, nc.scalar.copy)
+        project(1, 0, HALF, nc.scalar.copy)
+        project(0, HALF, P, nc.scalar.copy)
+        project(0, HALF + P, P, nc.vector.tensor_copy)
+        project(1, HALF, HALF, nc.scalar.copy)
+        for t in ORDER[2:]:
+            for c in range(2):
+                project(t, HALF * c, HALF, nc.scalar.copy)
 
         w2_g = sb("w2_g", [P, N, PACK], BF16)
-        nc.scalar.copy(w2_g[:].rearrange("p (c i) j -> p c j i", i=4), w2_raw[:].rearrange("p j (c i) -> p c j i", i=4))
-        w2_c = sb("w2_c", [P, N], U32)
-        w2_e = sb("w2_e", [P, N], U8)
+        for c in range(4):
+            cols = slice(P * c, P * (c + 1))
+            nc.scalar.copy(w2_g[:, cols, :].rearrange("p (c i) j -> p c j i", i=4), w2_raw[:, :, cols].rearrange("p j (c i) -> p c j i", i=4))
 
-        m1 = [sb("m1_%d" % t, [P, V], F32) for t in range(PACK)]
+        m1 = [None] * PACK
         ms = [sb("ms_%d" % t, [P, V], F32) for t in range(PACK)]
         md = [sb("md_%d" % t, [P, V], F32) for t in range(PACK)]
+        early = sb("early", [P, 2 * S], F32)
         pair = sb("pair", [P, 2 * S], F32)
-        zb = [sb("zb%d" % c, [P, HALF, PACK], BF16) for c in range(2)]
+        zb = [sb("zb%d" % c, [P, width, PACK], BF16) for c, (start, width) in enumerate(CHUNKS)]
 
         def fetch1(t):
+            m1[t] = sb("m1_%d" % t, [P, V], F32)
             nc.vector.tensor_copy(m1[t][:], state[t][:].indirect(s1_t[:]))
 
         def put1(t):
@@ -126,39 +132,50 @@ def tile_picked_carry2_none_p_kernel(tc, x_words, x_scales, w1, w2, offs, s1, d1
             window = pair if t == 2 else state[t]
             nc.vector.tensor_tensor(window[:].indirect(d2_t[:]), ms[t][:], md[t][:], ADD)
             if t < 2:
-                for c in range(2):
-                    nc.scalar.copy(zb[c][:, :, t], state[t][:, HALF * c : HALF * (c + 1)])
+                nc.scalar.copy(early[:, S * t : S * (t + 1)], state[t][:])
+            if t == 1:
+                early_v = early[:].rearrange("p (s j) -> p j s", s=2)
+                for c, (start, width) in enumerate(CHUNKS):
+                    nc.scalar.copy(zb[c][:, :, 0:2], early_v[:, start : start + width, :])
             if t == 3:
                 nc.scalar.copy(pair[:, S : 2 * S], state[t][:])
 
         fetch1(ORDER[0])
+        fetch1(ORDER[1])
         put1(ORDER[0])
         for i in range(PACK):
-            t = ORDER[i]
-            if i + 1 < PACK:
-                fetch1(ORDER[i + 1])
-            fetch2(t)
+            if i + 2 < PACK:
+                fetch1(ORDER[i + 2])
+            fetch2(ORDER[i])
             if i + 1 < PACK:
                 put1(ORDER[i + 1])
             else:
+                w2_c = sb("w2_c", [P, N], U32, tag="m1_%d" % ORDER[i])
+                w2_e = sb("w2_e", [P, N], U8)
                 nc.vector.quantize_mx(out=w2_c[:].bitcast(FP8X4), scales=w2_e[:], in_=w2_g[:].rearrange("p c j -> p (c j)"))
-            put2(t)
+            put2(ORDER[i])
 
         pair_v = pair[:].rearrange("p (s j) -> p j s", s=2)
-        z_c = [sb("z_c%d" % c, [P, HALF], U32) for c in range(2)]
-        z_e = [sb("z_e%d" % c, [P, HALF], U8) for c in range(2)]
-        nc.vector.tensor_copy(zb[0][:, :, 2:4], pair_v[:, 0:HALF, :])
-        nc.scalar.copy(zb[1][:, :, 2:4], pair_v[:, HALF:S, :])
-        for c in range(2):
+        z_c = [sb("z_c%d" % c, [P, width], U32) for c, (start, width) in enumerate(CHUNKS)]
+        z_e = [sb("z_e%d" % c, [P, width], U8) for c, (start, width) in enumerate(CHUNKS)]
+        for c, (start, width) in enumerate(CHUNKS):
+            copy = nc.scalar.copy if width == HALF else nc.vector.tensor_copy
+            copy(zb[c][:, :, 2:4], pair_v[:, start : start + width, :])
+        for c in range(len(CHUNKS)):
             nc.vector.quantize_mx(out=z_c[c][:].bitcast(FP8X4), scales=z_e[c][:], in_=zb[c][:].rearrange("p n j -> p (n j)"))
-        for c in range(2):
-            for b in range(PACK):
-                rows = slice(P * b, P * (b + 1))
-                acc = psum.tile([P, HALF], F32, name="acc")
-                nc.tensor.matmul_mx(out=acc[:], lhsT=w2_c[:, rows].bitcast(FP8X4), lhsT_scale=w2_e[:, rows], rhs=z_c[c][:].bitcast(FP8X4), rhs_scale=z_e[c][:], start=True, stop=True)
-                res = sb("res%d_%d" % (c, b), [P, HALF], F32)
-                if b % 2 == 0:
+        out_v = out.rearrange("(b p) j -> p b j", p=P)
+        turn = 0
+        for c, (start, width) in enumerate(CHUNKS):
+            per = HALF // width
+            for b0 in range(0, PACK, per):
+                acc = psum.tile([P, per, width], F32, name="acc")
+                for b in range(per):
+                    rows = slice(P * (b0 + b), P * (b0 + b + 1))
+                    nc.tensor.matmul_mx(out=acc[:, b, :], lhsT=w2_c[:, rows].bitcast(FP8X4), lhsT_scale=w2_e[:, rows], rhs=z_c[c][:].bitcast(FP8X4), rhs_scale=z_e[c][:], start=True, stop=True)
+                res = sb("res%d_%d" % (c, b0), [P, per, width], F32)
+                if turn % 2 == 0:
                     nc.scalar.copy(res[:], acc[:])
                 else:
                     nc.vector.tensor_copy(res[:], acc[:])
-                nc.sync.dma_start(out[rows, HALF * c : HALF * (c + 1)], res[:])
+                turn = turn + 1
+                nc.sync.dma_start(out_v[:, b0 : b0 + per, start : start + width], res[:])

@@ -154,6 +154,9 @@ def tile_picked_carry2_none_p_kernel(tc, x_words, x_scales, w1, w2, offs, s1, d1
                 w2_e = sb("w2_e", [P, N], U8)
                 nc.vector.quantize_mx(out=w2_c[:].bitcast(FP8X4), scales=w2_e[:], in_=w2_g[:].rearrange("p c j -> p (c j)"))
             put2(ORDER[i])
+        for b in range(2):
+            warm = psum.tile([P, N], F32, name="acc")
+            nc.tensor.matmul_mx(out=warm[:], lhsT=w2_c[:, 0:P].bitcast(FP8X4), lhsT_scale=w2_e[:, 0:P], rhs=w2_c[:].bitcast(FP8X4), rhs_scale=w2_e[:], start=True, stop=True)
 
         pair_v = pair[:].rearrange("p (s j) -> p j s", s=2)
         z_c = [sb("z_c%d" % c, [P, width], U32) for c, (start, width) in enumerate(CHUNKS)]

@@ -14,6 +14,7 @@ U8 = mybir.dt.uint8
 FP8X4 = mybir.dt.float8_e4m3fn_x4
 MULT = mybir.AluOpType.mult
 ADD = mybir.AluOpType.add
+COPY = mybir.ActivationFunctionType.Copy
 
 P = 128
 PACK = 4
@@ -41,7 +42,7 @@ def tile_picked_carry2_none_p_kernel(tc, x_words, x_scales, w1, w2, offs, s1, d1
         xs = sb("xs", [P, T], U8)
         nc.vector.memset(xs[:].bitcast(I32), 0)
         xw = sb("xw", [P, T], U32)
-        w1_raw = sb("w1_raw", [P, PACK, H], F32)
+        w1_raw = [sb("w1_raw%d" % e, [P, 2, H], F32) for e in range(2)]
         w2_raw = sb("w2_raw", [P, PACK, N], F32)
 
         def ld_sc(eng):
@@ -51,12 +52,13 @@ def tile_picked_carry2_none_p_kernel(tc, x_words, x_scales, w1, w2, offs, s1, d1
         def ld_x():
             nc.sync.dma_start(xw[:].bitcast(I32), x_words[0].rearrange("p n t -> p (n t)").bitcast(I32))
 
-        nc.sync.dma_start(w1_raw[:], w1.rearrange("(p j) c -> p j c", j=PACK))
+        w1_v = w1.rearrange("(p j) c -> p j c", j=PACK)
+        nc.sync.dma_start(w1_raw[0][:], w1_v[:, 0:2, :])
         nc.sync.dma_start(offs_t[:], offs)
-        nc.sync.dma_start(s1_t[:], s1)
         ld_sc(nc.sync)
+        nc.sync.dma_start(w1_raw[1][:], w1_v[:, 2:4, :])
         ld_x()
-        for tile, src in ((d1_t, d1), (s2_t, s2), (d2_t, d2)):
+        for tile, src in ((s1_t, s1), (d1_t, d1), (s2_t, s2), (d2_t, d2)):
             nc.sync.dma_start(tile[:], src)
         nc.sync.dma_start(w2_raw[:], w2.rearrange("(p j) c -> p j c", j=PACK))
 
@@ -65,11 +67,12 @@ def tile_picked_carry2_none_p_kernel(tc, x_words, x_scales, w1, w2, offs, s1, d1
         w1_e = [sb("w1_e%d" % u, [P, 2 * P], U8) for u in range(2)]
 
         def w1_weave(copy, u):
-            src = w1_raw[:].rearrange("p j (m t) -> p m j t", t=PACK)[:, :, :, 2 * u : 2 * u + 2]
-            copy(w1_g[u][:].rearrange("p t m j -> p m j t"), src)
+            for e in range(2):
+                src = w1_raw[e][:].rearrange("p j (m t) -> p m j t", t=PACK)[:, :, :, 2 * u : 2 * u + 2]
+                copy(w1_g[u][:, :, :, 2 * e : 2 * e + 2].rearrange("p t m j -> p m j t"), src)
 
         def w1_quant(u):
-            w1_c[u] = sb("w1_c%d" % u, [P, 2 * P], U32, tag="xw" if u == 1 else None)
+            w1_c[u] = sb("w1_c%d" % u, [P, 2 * P], U32)
             nc.vector.quantize_mx(out=w1_c[u][:].bitcast(FP8X4), scales=w1_e[u][:], in_=w1_g[u][:].rearrange("p t m j -> p (t m j)"))
 
         xg_s = sb("xg_s", [P, S], U8)
@@ -79,9 +82,9 @@ def tile_picked_carry2_none_p_kernel(tc, x_words, x_scales, w1, w2, offs, s1, d1
         w1_weave(nc.scalar.copy, 1)
         nc.vector.tensor_copy(xg_s[:], xs[:].indirect(offs_t[:]))
         w1_quant(0)
+        w1_quant(1)
         for c in range(2):
             nc.vector.tensor_copy(xg_w[c][:], xw[:].indirect(offs_t[:, 16 * c : 16 * (c + 1)]))
-        w1_quant(1)
 
         state = [sb("state%d" % t, [P, S], F32) for t in range(PACK)]
 
@@ -95,38 +98,46 @@ def tile_picked_carry2_none_p_kernel(tc, x_words, x_scales, w1, w2, offs, s1, d1
             copy(state[t][:, cols], acc[:])
 
         project(0, 0, HALF, nc.scalar.copy)
-        project(1, 0, HALF, nc.scalar.copy)
-        project(0, HALF, P, nc.scalar.copy)
-        project(0, HALF + P, P, nc.vector.tensor_copy)
+        project(1, 0, HALF, nc.vector.tensor_copy)
+        project(0, HALF, P, nc.vector.tensor_copy)
+        project(0, HALF + P, P, nc.scalar.copy)
         project(1, HALF, HALF, nc.scalar.copy)
+
+        def halve(dst, src):
+            nc.scalar.activation(dst, src, COPY, scale=0.5)
+
         for t in ORDER[2:]:
             for c in range(2):
-                project(t, HALF * c, HALF, nc.scalar.copy)
+                project(t, HALF * c, HALF, halve if t == 2 else nc.scalar.copy)
 
-        w2_g = sb("w2_g", [P, N, PACK], BF16)
+        w2_g = [sb("w2_g%d" % u, [P, HALF, PACK], BF16) for u in range(2)]
         for c in range(4):
             cols = slice(P * c, P * (c + 1))
-            nc.scalar.copy(w2_g[:, cols, :].rearrange("p (c i) j -> p c j i", i=4), w2_raw[:, :, cols].rearrange("p j (c i) -> p c j i", i=4))
+            nc.scalar.copy(w2_g[c // 2][:, P * (c % 2) : P * (c % 2 + 1), :].rearrange("p (c i) j -> p c j i", i=4), w2_raw[:, :, cols].rearrange("p j (c i) -> p c j i", i=4))
 
         m1 = [None] * PACK
         ms = [sb("ms_%d" % t, [P, V], F32) for t in range(PACK)]
         md = [sb("md_%d" % t, [P, V], F32) for t in range(PACK)]
         early = sb("early", [P, 2 * S], F32)
-        pair = sb("pair", [P, 2 * S], F32)
+        pair = sb("pair", [P, 2 * S], F32, tag="early")
         zb = [sb("zb%d" % c, [P, width, PACK], BF16) for c, (start, width) in enumerate(CHUNKS)]
 
         def fetch1(t):
-            m1[t] = sb("m1_%d" % t, [P, V], F32)
+            m1[t] = sb("m1_%d" % t, [P, V], F32, tag={ORDER[2]: "m1_%d" % ORDER[1], ORDER[3]: "ms_%d" % ORDER[1]}.get(t))
             nc.vector.tensor_copy(m1[t][:], state[t][:].indirect(s1_t[:]))
 
         def put1(t):
             nc.vector.tensor_copy(state[t][:].indirect(d1_t[:]), m1[t][:])
             if t == 2:
-                nc.scalar.copy(pair[:, 0:S], state[t][:])
+                nc.scalar.activation(pair[:, 0:S], state[t][:], COPY, scale=2.0)
 
         def fetch2(t):
-            nc.vector.tensor_scalar(ms[t][:], state[t][:].indirect(s2_t[:]), 0.5, 0.0, op0=MULT, op1=ADD)
-            nc.vector.tensor_scalar(md[t][:], state[t][:].indirect(d2_t[:]), 0.5, 0.0, op0=MULT, op1=ADD)
+            if t != 2:
+                nc.vector.tensor_scalar(ms[t][:], state[t][:].indirect(s2_t[:]), 0.5, 0.0, op0=MULT, op1=ADD)
+                nc.vector.tensor_scalar(md[t][:], state[t][:].indirect(d2_t[:]), 0.5, 0.0, op0=MULT, op1=ADD)
+            else:
+                nc.vector.tensor_copy(ms[t][:], state[t][:].indirect(s2_t[:]))
+                nc.vector.tensor_copy(md[t][:], state[t][:].indirect(d2_t[:]))
 
         def put2(t):
             window = pair if t == 2 else state[t]
@@ -140,45 +151,73 @@ def tile_picked_carry2_none_p_kernel(tc, x_words, x_scales, w1, w2, offs, s1, d1
             if t == 3:
                 nc.scalar.copy(pair[:, S : 2 * S], state[t][:])
 
-        fetch1(ORDER[0])
-        fetch1(ORDER[1])
-        put1(ORDER[0])
-        for i in range(PACK):
-            if i + 2 < PACK:
-                fetch1(ORDER[i + 2])
-            fetch2(ORDER[i])
-            if i + 1 < PACK:
-                put1(ORDER[i + 1])
-            else:
-                w2_c = sb("w2_c", [P, N], U32, tag="m1_%d" % ORDER[i])
-                w2_e = sb("w2_e", [P, N], U8)
-                nc.vector.quantize_mx(out=w2_c[:].bitcast(FP8X4), scales=w2_e[:], in_=w2_g[:].rearrange("p c j -> p (c j)"))
-            put2(ORDER[i])
-        for b in range(2):
-            warm = psum.tile([P, N], F32, name="acc")
-            nc.tensor.matmul_mx(out=warm[:], lhsT=w2_c[:, 0:P].bitcast(FP8X4), lhsT_scale=w2_e[:, 0:P], rhs=w2_c[:].bitcast(FP8X4), rhs_scale=w2_e[:], start=True, stop=True)
+        a, b, c, d = ORDER
+        fetch1(a)
+        fetch1(b)
+        put1(a)
+        put1(b)
+        fetch2(a)
+        fetch2(b)
+        put2(a)
+        fetch1(c)
+        put2(b)
+        put1(c)
+        fetch1(d)
+        fetch2(c)
+        put1(d)
+        put2(c)
+        fetch2(d)
+        w2_c = [None, None]
+        w2_e = [sb("w2_e%d" % u, [P, HALF], U8) for u in range(2)]
+
+        def w2_quant(u, tag):
+            w2_c[u] = sb("w2_c%d" % u, [P, HALF], U32, tag=tag)
+            nc.vector.quantize_mx(out=w2_c[u][:].bitcast(FP8X4), scales=w2_e[u][:], in_=w2_g[u][:].rearrange("p c j -> p (c j)"))
+
+        w2_quant(0, "ms_%d" % c)
+        put2(d)
 
         pair_v = pair[:].rearrange("p (s j) -> p j s", s=2)
         z_c = [sb("z_c%d" % c, [P, width], U32) for c, (start, width) in enumerate(CHUNKS)]
         z_e = [sb("z_e%d" % c, [P, width], U8) for c, (start, width) in enumerate(CHUNKS)]
-        for c, (start, width) in enumerate(CHUNKS):
-            copy = nc.scalar.copy if width == HALF else nc.vector.tensor_copy
-            copy(zb[c][:, :, 2:4], pair_v[:, start : start + width, :])
-        for c in range(len(CHUNKS)):
+
+        def z_quant(c):
             nc.vector.quantize_mx(out=z_c[c][:].bitcast(FP8X4), scales=z_e[c][:], in_=zb[c][:].rearrange("p n j -> p (n j)"))
+
+        nc.vector.tensor_copy(zb[0][:, :, 2:4], pair_v[:, 0:P, :])
+        nc.vector.tensor_copy(zb[1][:, :, 2:4], pair_v[:, P : 2 * P, :])
+        nc.scalar.copy(zb[2][:, :, 2:4], pair_v[:, 2 * P : 4 * P, :])
+        z_quant(0)
+        z_quant(1)
+        z_quant(2)
+        w2_quant(1, "zb1")
+
         out_v = out.rearrange("(b p) j -> p b j", p=P)
-        turn = 0
-        for c, (start, width) in enumerate(CHUNKS):
-            per = HALF // width
-            for b0 in range(0, PACK, per):
-                acc = psum.tile([P, per, width], F32, name="acc")
-                for b in range(per):
-                    rows = slice(P * (b0 + b), P * (b0 + b + 1))
-                    nc.tensor.matmul_mx(out=acc[:, b, :], lhsT=w2_c[:, rows].bitcast(FP8X4), lhsT_scale=w2_e[:, rows], rhs=z_c[c][:].bitcast(FP8X4), rhs_scale=z_e[c][:], start=True, stop=True)
-                res = sb("res%d_%d" % (c, b0), [P, per, width], F32)
-                if turn % 2 == 0:
-                    nc.scalar.copy(res[:], acc[:])
-                else:
-                    nc.vector.tensor_copy(res[:], acc[:])
-                turn = turn + 1
-                nc.sync.dma_start(out_v[:, b0 : b0 + per, start : start + width], res[:])
+
+        def product(acc, b, n):
+            rows = slice(P * (b % 2), P * (b % 2 + 1))
+            nc.tensor.matmul_mx(out=acc, lhsT=w2_c[b // 2][:, rows].bitcast(FP8X4), lhsT_scale=w2_e[b // 2][:, rows], rhs=z_c[n][:].bitcast(FP8X4), rhs_scale=z_e[n][:], start=True, stop=True)
+
+        def piece(b, chunks, copy, res):
+            start = CHUNKS[chunks[0]][0]
+            width = sum(CHUNKS[n][1] for n in chunks)
+            acc = psum.tile([P, width], F32, name="acc")
+            for n in chunks:
+                product(acc[:, CHUNKS[n][0] - start : CHUNKS[n][0] - start + CHUNKS[n][1]], b, n)
+            copy(res, acc[:])
+
+        def stored(b, chunks, copy, tag=None):
+            start = CHUNKS[chunks[0]][0]
+            width = sum(CHUNKS[n][1] for n in chunks)
+            res = sb("res%d_%d" % (b, start), [P, width], F32, tag=tag)
+            piece(b, chunks, copy, res[:])
+            nc.sync.dma_start(out_v[:, b, start : start + width], res[:])
+
+        stored(0, (0,), nc.scalar.copy)
+        stored(1, (0, 1), nc.vector.tensor_copy, tag="w2_g1")
+        stored(0, (1,), nc.scalar.copy)
+        stored(0, (2,), nc.scalar.copy)
+        stored(1, (2,), nc.vector.tensor_copy)
+        for b in range(2, PACK):
+            stored(b, (0, 1), nc.scalar.copy)
+            stored(b, (2,), nc.vector.tensor_copy)

@@ -43,11 +43,9 @@ def tile_picked_carry2_none_p_kernel(tc, x_words, x_scales, w1, w2, offs, s1, d1
         nc.vector.memset(xs[:].bitcast(I32), 0)
         xw = sb("xw", [P, T], U32)
         w1_raw = [sb("w1_raw%d" % e, [P, 2, H], F32) for e in range(2)]
-        w2_raw = sb("w2_raw", [P, PACK, N], F32)
 
         def ld_sc(eng):
-            for q in range(4):
-                eng.dma_start(xs[32 * q : 32 * q + 4, :].bitcast(I32), x_scales[0, 4 * q : 4 * q + 4, :].bitcast(I32))
+            eng.dma_start(xs[0:P:8, :].bitcast(I32), x_scales[0].bitcast(I32))
 
         def ld_x():
             nc.sync.dma_start(xw[:].bitcast(I32), x_words[0].rearrange("p n t -> p (n t)").bitcast(I32))
@@ -60,7 +58,6 @@ def tile_picked_carry2_none_p_kernel(tc, x_words, x_scales, w1, w2, offs, s1, d1
         ld_x()
         for tile, src in ((s1_t, s1), (d1_t, d1), (s2_t, s2), (d2_t, d2)):
             nc.sync.dma_start(tile[:], src)
-        nc.sync.dma_start(w2_raw[:], w2.rearrange("(p j) c -> p j c", j=PACK))
 
         w1_g = [sb("w1_g%d" % u, [P, 2, P, PACK], BF16) for u in range(2)]
         w1_c = [None, None]
@@ -80,7 +77,13 @@ def tile_picked_carry2_none_p_kernel(tc, x_words, x_scales, w1, w2, offs, s1, d1
 
         w1_weave(nc.vector.tensor_copy, 0)
         w1_weave(nc.scalar.copy, 1)
-        nc.vector.tensor_copy(xg_s[:], xs[:].indirect(offs_t[:]))
+        spread = sb("spread", [P, S], U8)
+        nc.vector.tensor_copy(spread[:], xs[:].indirect(offs_t[:]))
+        nc.vector.tensor_copy(xg_s[:].bitcast(I32), spread[:].bitcast(I32))
+        for r in range(1, 4):
+            nc.scalar.dma_start(xg_s[r:P:32, :].bitcast(I32), spread[8 * r : P : 32, :].bitcast(I32))
+        w2_raw = sb("w2_raw", [P, PACK, N], F32, tag="spread")
+        nc.sync.dma_start(w2_raw[:], w2.rearrange("(p j) c -> p j c", j=PACK))
         w1_quant(0)
         w1_quant(1)
         for c in range(2):

@@ -28,7 +28,11 @@ def tile_picked_carry2_none_p_kernel(tc, x_words, x_scales, w1, w2, offs, s1, d1
     with ExitStack() as ctx:
         lists = ctx.enter_context(tc.tile_pool(name="lists", bufs=1))
         keep = ctx.enter_context(tc.tile_pool(name="keep", bufs=1))
+        shared = ctx.enter_context(tc.tile_pool(name="shared", bufs=1))
         psum = ctx.enter_context(tc.psum_pool(name="psum", bufs=8))
+
+        def at(name, shape, dtype, offset):
+            return shared.tile(shape, dtype, name=name, tag=name, align_bytes=64, offset=offset)
 
         def sb(name, shape, dtype, tag=None):
             return keep.tile(shape, dtype, name=name, tag=tag or name, align_bytes=64)
@@ -63,10 +67,9 @@ def tile_picked_carry2_none_p_kernel(tc, x_words, x_scales, w1, w2, offs, s1, d1
         w1_c = [None, None]
         w1_e = [sb("w1_e%d" % u, [P, 2 * P], U8) for u in range(2)]
 
-        def w1_weave(copy, u):
-            for e in range(2):
-                src = w1_raw[e][:].rearrange("p j (m t) -> p m j t", t=PACK)[:, :, :, 2 * u : 2 * u + 2]
-                copy(w1_g[u][:, :, :, 2 * e : 2 * e + 2].rearrange("p t m j -> p m j t"), src)
+        def w1_weave(copy, u, e):
+            src = w1_raw[e][:].rearrange("p j (m t) -> p m j t", t=PACK)[:, :, :, 2 * u : 2 * u + 2]
+            copy(w1_g[u][:, :, :, 2 * e : 2 * e + 2].rearrange("p t m j -> p m j t"), src)
 
         def w1_quant(u):
             w1_c[u] = sb("w1_c%d" % u, [P, 2 * P], U32)
@@ -75,13 +78,15 @@ def tile_picked_carry2_none_p_kernel(tc, x_words, x_scales, w1, w2, offs, s1, d1
         xg_s = sb("xg_s", [P, S], U8)
         xg_w = [sb("xg_w%d" % c, [P, HALF], U32) for c in range(2)]
 
-        w1_weave(nc.vector.tensor_copy, 0)
-        w1_weave(nc.scalar.copy, 1)
+        w1_weave(nc.scalar.copy, 0, 0)
+        w1_weave(nc.scalar.copy, 1, 0)
         spread = sb("spread", [P, S], U8)
         nc.vector.tensor_copy(spread[:], xs[:].indirect(offs_t[:]))
         nc.vector.tensor_copy(xg_s[:].bitcast(I32), spread[:].bitcast(I32))
         for r in range(1, 4):
             nc.scalar.dma_start(xg_s[r:P:32, :].bitcast(I32), spread[8 * r : P : 32, :].bitcast(I32))
+        w1_weave(nc.vector.tensor_copy, 0, 1)
+        w1_weave(nc.scalar.copy, 1, 1)
         w2_raw = sb("w2_raw", [P, PACK, N], F32, tag="spread")
         nc.sync.dma_start(w2_raw[:], w2.rearrange("(p j) c -> p j c", j=PACK))
         w1_quant(0)
@@ -113,24 +118,28 @@ def tile_picked_carry2_none_p_kernel(tc, x_words, x_scales, w1, w2, offs, s1, d1
             for c in range(2):
                 project(t, HALF * c, HALF, halve if t == 2 else nc.scalar.copy)
 
-        w2_g = [sb("w2_g%d" % u, [P, HALF, PACK], BF16) for u in range(2)]
+        w2_g = [sb("w2_g%d" % u, [P, width, PACK], BF16) for u, (start, width) in enumerate(CHUNKS)]
         for c in range(4):
             cols = slice(P * c, P * (c + 1))
-            nc.scalar.copy(w2_g[c // 2][:, P * (c % 2) : P * (c % 2 + 1), :].rearrange("p (c i) j -> p c j i", i=4), w2_raw[:, :, cols].rearrange("p j (c i) -> p c j i", i=4))
+            dst = w2_g[c][:] if c < 2 else w2_g[2][:, P * (c - 2) : P * (c - 1), :]
+            nc.scalar.copy(dst.rearrange("p (c i) j -> p c j i", i=4), w2_raw[:, :, cols].rearrange("p j (c i) -> p c j i", i=4))
 
         m1 = [None] * PACK
         ms = [sb("ms_%d" % t, [P, V], F32) for t in range(PACK)]
         md = [sb("md_%d" % t, [P, V], F32) for t in range(PACK)]
         early = sb("early", [P, 2 * S], F32)
         pair = sb("pair", [P, 2 * S], F32, tag="early")
-        zb = [sb("zb%d" % c, [P, width, PACK], BF16) for c, (start, width) in enumerate(CHUNKS)]
+        zb = [at("zb%d" % c, [P, width, PACK], BF16, 2 * PACK * start) for c, (start, width) in enumerate(CHUNKS)]
 
         def fetch1(t):
-            m1[t] = sb("m1_%d" % t, [P, V], F32, tag={ORDER[2]: "m1_%d" % ORDER[1], ORDER[3]: "ms_%d" % ORDER[1]}.get(t))
-            nc.vector.tensor_copy(m1[t][:], state[t][:].indirect(s1_t[:]))
+            if t in ORDER[1:3]:
+                m1[t] = at("m1_%d" % t, [P, V + 32], F32, 960)[:, 0:V]
+            else:
+                m1[t] = sb("m1_%d" % t, [P, V], F32, tag={ORDER[3]: "ms_%d" % ORDER[1]}.get(t))[:]
+            nc.vector.tensor_copy(m1[t], state[t][:].indirect(s1_t[:]))
 
         def put1(t):
-            nc.vector.tensor_copy(state[t][:].indirect(d1_t[:]), m1[t][:])
+            nc.vector.tensor_copy(state[t][:].indirect(d1_t[:]), m1[t])
             if t == 2:
                 nc.scalar.activation(pair[:, 0:S], state[t][:], COPY, scale=2.0)
 
@@ -170,57 +179,53 @@ def tile_picked_carry2_none_p_kernel(tc, x_words, x_scales, w1, w2, offs, s1, d1
         put1(d)
         put2(c)
         fetch2(d)
-        w2_c = [None, None]
-        w2_e = [sb("w2_e%d" % u, [P, HALF], U8) for u in range(2)]
+        w2_c = [None] * len(CHUNKS)
+        w2_e = [sb("w2_e%d" % u, [P, width], U8) for u, (start, width) in enumerate(CHUNKS)]
 
-        def w2_quant(u, tag):
-            w2_c[u] = sb("w2_c%d" % u, [P, HALF], U32, tag=tag)
-            nc.vector.quantize_mx(out=w2_c[u][:].bitcast(FP8X4), scales=w2_e[u][:], in_=w2_g[u][:].rearrange("p c j -> p (c j)"))
+        def w2_quant(u, codes):
+            w2_c[u] = codes
+            nc.vector.quantize_mx(out=codes[:].bitcast(FP8X4), scales=w2_e[u][:], in_=w2_g[u][:].rearrange("p c j -> p (c j)"))
 
-        w2_quant(0, "ms_%d" % c)
+        w2_quant(0, sb("w2_c0", [P, P], U32, tag="ms_%d" % c))
         put2(d)
 
         pair_v = pair[:].rearrange("p (s j) -> p j s", s=2)
-        z_c = [sb("z_c%d" % c, [P, width], U32) for c, (start, width) in enumerate(CHUNKS)]
-        z_e = [sb("z_e%d" % c, [P, width], U8) for c, (start, width) in enumerate(CHUNKS)]
+        z_c = [sb("z_c%d" % h, [P, HALF], U32) for h in range(2)]
+        z_e = [sb("z_e%d" % h, [P, HALF], U8) for h in range(2)]
+
+        def z_round(c, copy):
+            start, width = CHUNKS[c]
+            copy(zb[c][:, :, 2:4], pair_v[:, start : start + width, :])
 
         def z_quant(c):
-            nc.vector.quantize_mx(out=z_c[c][:].bitcast(FP8X4), scales=z_e[c][:], in_=zb[c][:].rearrange("p n j -> p (n j)"))
+            start, width = CHUNKS[c]
+            cols = slice(start % HALF, start % HALF + width)
+            nc.vector.quantize_mx(out=z_c[start // HALF][:, cols].bitcast(FP8X4), scales=z_e[start // HALF][:, cols], in_=zb[c][:].rearrange("p n j -> p (n j)"))
 
-        nc.vector.tensor_copy(zb[0][:, :, 2:4], pair_v[:, 0:P, :])
-        nc.vector.tensor_copy(zb[1][:, :, 2:4], pair_v[:, P : 2 * P, :])
-        nc.scalar.copy(zb[2][:, :, 2:4], pair_v[:, 2 * P : 4 * P, :])
+        z_round(0, nc.vector.tensor_copy)
+        z_round(1, nc.vector.tensor_copy)
+        z_round(2, nc.scalar.copy)
+        w2_quant(1, sb("w2_c1", [P, P], U32, tag="state%d" % c))
         z_quant(0)
         z_quant(1)
+        w2_quant(2, at("w2_c2", [P, HALF], U32, 0))
         z_quant(2)
-        w2_quant(1, "zb1")
 
         out_v = out.rearrange("(b p) j -> p b j", p=P)
 
-        def product(acc, b, n):
-            rows = slice(P * (b % 2), P * (b % 2 + 1))
-            nc.tensor.matmul_mx(out=acc, lhsT=w2_c[b // 2][:, rows].bitcast(FP8X4), lhsT_scale=w2_e[b // 2][:, rows], rhs=z_c[n][:].bitcast(FP8X4), rhs_scale=z_e[n][:], start=True, stop=True)
-
-        def piece(b, chunks, copy, res):
-            start = CHUNKS[chunks[0]][0]
-            width = sum(CHUNKS[n][1] for n in chunks)
+        def stored(b, start, width, copy):
+            u = min(b, 2)
+            rows = slice(P * (b - u), P * (b - u + 1))
+            cols = slice(start % HALF, start % HALF + width)
             acc = psum.tile([P, width], F32, name="acc")
-            for n in chunks:
-                product(acc[:, CHUNKS[n][0] - start : CHUNKS[n][0] - start + CHUNKS[n][1]], b, n)
-            copy(res, acc[:])
-
-        def stored(b, chunks, copy, tag=None):
-            start = CHUNKS[chunks[0]][0]
-            width = sum(CHUNKS[n][1] for n in chunks)
-            res = sb("res%d_%d" % (b, start), [P, width], F32, tag=tag)
-            piece(b, chunks, copy, res[:])
+            nc.tensor.matmul_mx(out=acc[:], lhsT=w2_c[u][:, rows].bitcast(FP8X4), lhsT_scale=w2_e[u][:, rows], rhs=z_c[start // HALF][:, cols].bitcast(FP8X4), rhs_scale=z_e[start // HALF][:, cols], start=True, stop=True)
+            res = sb("res%d_%d" % (b, start), [P, width], F32)
+            copy(res[:], acc[:])
             nc.sync.dma_start(out_v[:, b, start : start + width], res[:])
 
-        stored(0, (0,), nc.scalar.copy)
-        stored(1, (0, 1), nc.vector.tensor_copy, tag="w2_g1")
-        stored(0, (1,), nc.scalar.copy)
-        stored(0, (2,), nc.scalar.copy)
-        stored(1, (2,), nc.vector.tensor_copy)
-        for b in range(2, PACK):
-            stored(b, (0, 1), nc.scalar.copy)
-            stored(b, (2,), nc.vector.tensor_copy)
+        stored(0, 0, P, nc.scalar.copy)
+        stored(0, P, P, nc.scalar.copy)
+        for b in range(1, PACK):
+            stored(b, 0, HALF, nc.scalar.copy if b < 3 else nc.vector.tensor_copy)
+        for b in range(PACK):
+            stored(b, HALF, HALF, nc.vector.tensor_copy if b % 2 else nc.scalar.copy)

@@ -76,7 +76,8 @@ def tile_picked_carry2_none_p_kernel(tc, x_words, x_scales, w1, w2, offs, s1, d1
             nc.vector.quantize_mx(out=w1_c[u][:].bitcast(FP8X4), scales=w1_e[u][:], in_=w1_g[u][:].rearrange("p t m j -> p (t m j)"))
 
         xg_s = sb("xg_s", [P, S], U8)
-        xg_w = [sb("xg_w%d" % c, [P, HALF], U32) for c in range(2)]
+        xg_all = sb("xg_all", [P, S], U32)
+        xg_w = [xg_all[:, HALF * c : HALF * (c + 1)] for c in range(2)]
 
         w1_weave(nc.scalar.copy, 0, 0)
         w1_weave(nc.scalar.copy, 1, 0)
@@ -92,7 +93,7 @@ def tile_picked_carry2_none_p_kernel(tc, x_words, x_scales, w1, w2, offs, s1, d1
         w1_quant(0)
         w1_quant(1)
         for c in range(2):
-            nc.vector.tensor_copy(xg_w[c][:], xw[:].indirect(offs_t[:, 16 * c : 16 * (c + 1)]))
+            nc.vector.tensor_copy(xg_w[c], xw[:].indirect(offs_t[:, 16 * c : 16 * (c + 1)]))
 
         state = [sb("state%d" % t, [P, S], F32) for t in range(PACK)]
 
@@ -206,6 +207,8 @@ def tile_picked_carry2_none_p_kernel(tc, x_words, x_scales, w1, w2, offs, s1, d1
         z_round(1, nc.vector.tensor_copy)
         z_round(2, nc.scalar.copy)
         w2_quant(1, sb("w2_c1", [P, P], U32, tag="state%d" % c))
+        warm = psum.tile([P, S], F32, name="acc")
+        nc.tensor.matmul_mx(out=warm[:], lhsT=w2_c[1][:].bitcast(FP8X4), lhsT_scale=w2_e[1][:], rhs=xg_all[:].bitcast(FP8X4), rhs_scale=xg_s[:], start=True, stop=True)
         z_quant(0)
         z_quant(1)
         w2_quant(2, at("w2_c2", [P, HALF], U32, 0))
@@ -213,19 +216,26 @@ def tile_picked_carry2_none_p_kernel(tc, x_words, x_scales, w1, w2, offs, s1, d1
 
         out_v = out.rearrange("(b p) j -> p b j", p=P)
 
-        def stored(b, start, width, copy):
+        def piece(b, start, width, copy, res):
             u = min(b, 2)
             rows = slice(P * (b - u), P * (b - u + 1))
             cols = slice(start % HALF, start % HALF + width)
             acc = psum.tile([P, width], F32, name="acc")
             nc.tensor.matmul_mx(out=acc[:], lhsT=w2_c[u][:, rows].bitcast(FP8X4), lhsT_scale=w2_e[u][:, rows], rhs=z_c[start // HALF][:, cols].bitcast(FP8X4), rhs_scale=z_e[start // HALF][:, cols], start=True, stop=True)
+            copy(res, acc[:])
+
+        def stored(b, start, width, copy):
             res = sb("res%d_%d" % (b, start), [P, width], F32)
-            copy(res[:], acc[:])
+            piece(b, start, width, copy, res[:])
             nc.sync.dma_start(out_v[:, b, start : start + width], res[:])
 
         stored(0, 0, P, nc.scalar.copy)
         stored(0, P, P, nc.scalar.copy)
         for b in range(1, PACK):
             stored(b, 0, HALF, nc.scalar.copy if b < 3 else nc.vector.tensor_copy)
-        for b in range(PACK):
+        for b in range(PACK - 1):
             stored(b, HALF, HALF, nc.vector.tensor_copy if b % 2 else nc.scalar.copy)
+        last = sb("res_last", [P, HALF], F32)
+        piece(PACK - 1, HALF, P, nc.vector.tensor_copy, last[:, 0:P])
+        piece(PACK - 1, HALF + P, P, nc.vector.tensor_copy, last[:, P:HALF])
+        nc.sync.dma_start(out_v[:, PACK - 1, HALF:S], last[:])

@@ -188,6 +188,9 @@ def tile_picked_carry2_none_p_kernel(tc, x_words, x_scales, w1, w2, offs, s1, d1
             nc.vector.quantize_mx(out=codes[:].bitcast(FP8X4), scales=w2_e[u][:], in_=w2_g[u][:].rearrange("p c j -> p (c j)"))
 
         w2_quant(0, sb("w2_c0", [P, P], U32, tag="ms_%d" % c))
+        for n in range(2):
+            warm = psum.tile([P, S], F32, name="acc")
+            nc.tensor.matmul_mx(out=warm[:], lhsT=w2_c[0][:].bitcast(FP8X4), lhsT_scale=w2_e[0][:], rhs=xg_all[:].bitcast(FP8X4), rhs_scale=xg_s[:], start=True, stop=True)
         put2(d)
 
         pair_v = pair[:].rearrange("p (s j) -> p j s", s=2)
@@ -207,8 +210,6 @@ def tile_picked_carry2_none_p_kernel(tc, x_words, x_scales, w1, w2, offs, s1, d1
         z_round(1, nc.vector.tensor_copy)
         z_round(2, nc.scalar.copy)
         w2_quant(1, sb("w2_c1", [P, P], U32, tag="state%d" % c))
-        warm = psum.tile([P, S], F32, name="acc")
-        nc.tensor.matmul_mx(out=warm[:], lhsT=w2_c[1][:].bitcast(FP8X4), lhsT_scale=w2_e[1][:], rhs=xg_all[:].bitcast(FP8X4), rhs_scale=xg_s[:], start=True, stop=True)
         z_quant(0)
         z_quant(1)
         w2_quant(2, at("w2_c2", [P, HALF], U32, 0))
@@ -230,8 +231,12 @@ def tile_picked_carry2_none_p_kernel(tc, x_words, x_scales, w1, w2, offs, s1, d1
             nc.sync.dma_start(out_v[:, b, start : start + width], res[:])
 
         stored(0, 0, P, nc.scalar.copy)
+        second = sb("res_second", [P, HALF], F32)
+        piece(1, 0, P, nc.scalar.copy, second[:, 0:P])
         stored(0, P, P, nc.scalar.copy)
-        for b in range(1, PACK):
+        piece(1, P, P, nc.scalar.copy, second[:, P:HALF])
+        nc.sync.dma_start(out_v[:, 1, 0:HALF], second[:])
+        for b in range(2, PACK):
             stored(b, 0, HALF, nc.scalar.copy if b < 3 else nc.vector.tensor_copy)
         for b in range(PACK - 1):
             stored(b, HALF, HALF, nc.vector.tensor_copy if b % 2 else nc.scalar.copy)

@@ -14,13 +14,13 @@ U8 = mybir.dt.uint8
 FP8X4 = mybir.dt.float8_e4m3fn_x4
 MULT = mybir.AluOpType.mult
 ADD = mybir.AluOpType.add
-COPY = mybir.ActivationFunctionType.Copy
 
 P = 128
 PACK = 4
 HALF = 256
-ORDER = (0, 1, 3, 2)
-CHUNKS = ((0, 128), (128, 128), (256, 256))
+QUADRANT = 32
+SPREAD = 8
+PIECES = ((0, 128), (128, 128), (256, 256))
 
 
 def tile_picked_carry2_none_p_kernel(tc, x_words, x_scales, w1, w2, offs, s1, d1, s2, d2, out):
@@ -28,14 +28,18 @@ def tile_picked_carry2_none_p_kernel(tc, x_words, x_scales, w1, w2, offs, s1, d1
     with ExitStack() as ctx:
         lists = ctx.enter_context(tc.tile_pool(name="lists", bufs=1))
         keep = ctx.enter_context(tc.tile_pool(name="keep", bufs=1))
-        shared = ctx.enter_context(tc.tile_pool(name="shared", bufs=1))
         psum = ctx.enter_context(tc.psum_pool(name="psum", bufs=8))
 
-        def at(name, shape, dtype, offset):
-            return shared.tile(shape, dtype, name=name, tag=name, align_bytes=64, offset=offset)
+        def sbuf(name, shape, dtype, after=None):
+            return keep.tile(shape, dtype, name=name, tag=after or name, align_bytes=64)
 
-        def sb(name, shape, dtype, tag=None):
-            return keep.tile(shape, dtype, name=name, tag=tag or name, align_bytes=64)
+        def quantise(codes, scales, values):
+            nc.vector.quantize_mx(out=codes.bitcast(FP8X4), scales=scales, in_=values)
+
+        def product(codes_l, scales_l, codes_r, scales_r, width):
+            acc = psum.tile([P, width], F32, name="acc")
+            nc.tensor.matmul_mx(out=acc[:], lhsT=codes_l.bitcast(FP8X4), lhsT_scale=scales_l, rhs=codes_r.bitcast(FP8X4), rhs_scale=scales_r, start=True, stop=True)
+            return acc
 
         offs_t = lists.tile([P, S // 16], U16, name="offs_t")
         s1_t = lists.tile([P, V // 16], U16, name="s1_t")
@@ -43,204 +47,172 @@ def tile_picked_carry2_none_p_kernel(tc, x_words, x_scales, w1, w2, offs, s1, d1
         s2_t = lists.tile([P, V // 16], U16, name="s2_t")
         d2_t = lists.tile([P, V // 16], U16, name="d2_t")
 
-        xs = sb("xs", [P, T], U8)
-        nc.vector.memset(xs[:].bitcast(I32), 0)
-        xw = sb("xw", [P, T], U32)
-        w1_raw = [sb("w1_raw%d" % e, [P, 2, H], F32) for e in range(2)]
-
-        def ld_sc(eng):
-            eng.dma_start(xs[0:P:8, :].bitcast(I32), x_scales[0].bitcast(I32))
-
-        def ld_x():
-            nc.sync.dma_start(xw[:].bitcast(I32), x_words[0].rearrange("p n t -> p (n t)").bitcast(I32))
+        x_scale_rows = sbuf("x_scale_rows", [P, T], U8)
+        nc.vector.memset(x_scale_rows[:].bitcast(I32), 0)
+        x_word_rows = sbuf("x_word_rows", [P, T], U32)
+        w1_raw = [sbuf("w1_raw%d" % e, [P, 2, H], F32) for e in range(2)]
 
         w1_v = w1.rearrange("(p j) c -> p j c", j=PACK)
         nc.sync.dma_start(w1_raw[0][:], w1_v[:, 0:2, :])
         nc.sync.dma_start(offs_t[:], offs)
-        ld_sc(nc.sync)
+        nc.sync.dma_start(x_scale_rows[0:P:SPREAD, :].bitcast(I32), x_scales[0].bitcast(I32))
         nc.sync.dma_start(w1_raw[1][:], w1_v[:, 2:4, :])
-        ld_x()
+        nc.sync.dma_start(x_word_rows[:].bitcast(I32), x_words[0].rearrange("p n t -> p (n t)").bitcast(I32))
         for tile, src in ((s1_t, s1), (d1_t, d1), (s2_t, s2), (d2_t, d2)):
             nc.sync.dma_start(tile[:], src)
 
-        w1_g = [sb("w1_g%d" % u, [P, 2, P, PACK], BF16) for u in range(2)]
-        w1_c = [None, None]
-        w1_e = [sb("w1_e%d" % u, [P, 2 * P], U8) for u in range(2)]
+        w1_bf = [sbuf("w1_bf%d" % u, [P, 2, P, PACK], BF16) for u in range(2)]
+        w1_codes = [sbuf("w1_codes%d" % u, [P, 2 * P], U32) for u in range(2)]
+        w1_scales = [sbuf("w1_scales%d" % u, [P, 2 * P], U8) for u in range(2)]
 
-        def w1_weave(copy, u, e):
+        def lay_w1(u, e, copy):
             src = w1_raw[e][:].rearrange("p j (m t) -> p m j t", t=PACK)[:, :, :, 2 * u : 2 * u + 2]
-            copy(w1_g[u][:, :, :, 2 * e : 2 * e + 2].rearrange("p t m j -> p m j t"), src)
+            copy(w1_bf[u][:, :, :, 2 * e : 2 * e + 2].rearrange("p i m j -> p m j i"), src)
 
-        def w1_quant(u):
-            w1_c[u] = sb("w1_c%d" % u, [P, 2 * P], U32)
-            nc.vector.quantize_mx(out=w1_c[u][:].bitcast(FP8X4), scales=w1_e[u][:], in_=w1_g[u][:].rearrange("p t m j -> p (t m j)"))
+        x_scales_spread = sbuf("x_scales_spread", [P, S], U8)
+        x_scales_picked = sbuf("x_scales_picked", [P, S], U8)
+        x_words_picked = sbuf("x_words_picked", [P, S], U32)
 
-        xg_s = sb("xg_s", [P, S], U8)
-        xg_all = sb("xg_all", [P, S], U32)
-        xg_w = [xg_all[:, HALF * c : HALF * (c + 1)] for c in range(2)]
-
-        w1_weave(nc.scalar.copy, 0, 0)
-        w1_weave(nc.scalar.copy, 1, 0)
-        spread = sb("spread", [P, S], U8)
-        nc.vector.tensor_copy(spread[:], xs[:].indirect(offs_t[:]))
-        nc.vector.tensor_copy(xg_s[:].bitcast(I32), spread[:].bitcast(I32))
+        lay_w1(0, 0, nc.scalar.copy)
+        lay_w1(1, 0, nc.scalar.copy)
+        nc.vector.tensor_copy(x_scales_spread[:], x_scale_rows[:].indirect(offs_t[:]))
+        nc.vector.tensor_copy(x_scales_picked[:].bitcast(I32), x_scales_spread[:].bitcast(I32))
         for r in range(1, 4):
-            nc.scalar.dma_start(xg_s[r:P:32, :].bitcast(I32), spread[8 * r : P : 32, :].bitcast(I32))
-        w1_weave(nc.vector.tensor_copy, 0, 1)
-        w1_weave(nc.scalar.copy, 1, 1)
-        w2_raw = sb("w2_raw", [P, PACK, N], F32, tag="spread")
+            nc.scalar.dma_start(x_scales_picked[r:P:QUADRANT, :].bitcast(I32), x_scales_spread[SPREAD * r : P : QUADRANT, :].bitcast(I32))
+        lay_w1(0, 1, nc.vector.tensor_copy)
+        lay_w1(1, 1, nc.scalar.copy)
+        w2_raw = sbuf("w2_raw", [P, PACK, N], F32, after="x_scales_spread")
         nc.sync.dma_start(w2_raw[:], w2.rearrange("(p j) c -> p j c", j=PACK))
-        w1_quant(0)
-        w1_quant(1)
-        for c in range(2):
-            nc.vector.tensor_copy(xg_w[c], xw[:].indirect(offs_t[:, 16 * c : 16 * (c + 1)]))
+        for u in range(2):
+            quantise(w1_codes[u][:], w1_scales[u][:], w1_bf[u][:].rearrange("p i m j -> p (i m j)"))
+        for start in (0, HALF):
+            nc.vector.tensor_copy(x_words_picked[:, start : start + HALF], x_word_rows[:].indirect(offs_t[:, start // 16 : (start + HALF) // 16]))
 
-        state = [sb("state%d" % t, [P, S], F32) for t in range(PACK)]
+        plane = [sbuf("plane%d" % t, [P, S], F32) for t in range(PACK)]
 
         def project(t, start, width, copy):
-            cols = slice(start, start + width)
-            c = start // HALF
-            local = slice(start - HALF * c, start - HALF * c + width)
-            feats = slice(P * (t % 2), P * (t % 2 + 1))
-            acc = psum.tile([P, width], F32, name="acc")
-            nc.tensor.matmul_mx(out=acc[:], lhsT=w1_c[t // 2][:, feats].bitcast(FP8X4), lhsT_scale=w1_e[t // 2][:, feats], rhs=xg_w[c][:, local].bitcast(FP8X4), rhs_scale=xg_s[:, cols], start=True, stop=True)
-            copy(state[t][:, cols], acc[:])
+            places = slice(start, start + width)
+            columns = slice(P * (t % 2), P * (t % 2 + 1))
+            acc = product(w1_codes[t // 2][:, columns], w1_scales[t // 2][:, columns], x_words_picked[:, places], x_scales_picked[:, places], width)
+            copy(plane[t][:, places], acc[:])
 
         project(0, 0, HALF, nc.scalar.copy)
         project(1, 0, HALF, nc.vector.tensor_copy)
         project(0, HALF, P, nc.vector.tensor_copy)
         project(0, HALF + P, P, nc.scalar.copy)
         project(1, HALF, HALF, nc.scalar.copy)
+        for t in (3, 2):
+            for start in (0, HALF):
+                project(t, start, HALF, nc.scalar.copy)
 
-        def halve(dst, src):
-            nc.scalar.activation(dst, src, COPY, scale=0.5)
+        w2_bf = [sbuf("w2_bf%d" % n, [P, width, PACK], BF16) for n, (start, width) in enumerate(PIECES)]
+        for n, (start, width) in enumerate(PIECES):
+            for first in range(0, width, P):
+                src = w2_raw[:, :, start + first : start + first + P]
+                nc.scalar.copy(w2_bf[n][:, first : first + P, :].rearrange("p (c i) j -> p c j i", i=4), src.rearrange("p j (c i) -> p c j i", i=4))
 
-        for t in ORDER[2:]:
-            for c in range(2):
-                project(t, HALF * c, HALF, halve if t == 2 else nc.scalar.copy)
+        moved = [None] * PACK
+        half_s = [sbuf("half_s%d" % t, [P, V], F32) for t in range(PACK)]
+        half_d = [sbuf("half_d%d" % t, [P, V], F32) for t in range(PACK)]
+        pair01 = sbuf("pair01", [P, 2 * S], F32)
+        pair23 = sbuf("pair23", [P, 2 * S], F32, after="pair01")
+        z_bf = [sbuf("z_bf%d" % n, [P, width, PACK], BF16) for n, (start, width) in enumerate(PIECES)]
 
-        w2_g = [sb("w2_g%d" % u, [P, width, PACK], BF16) for u, (start, width) in enumerate(CHUNKS)]
-        for c in range(4):
-            cols = slice(P * c, P * (c + 1))
-            dst = w2_g[c][:] if c < 2 else w2_g[2][:, P * (c - 2) : P * (c - 1), :]
-            nc.scalar.copy(dst.rearrange("p (c i) j -> p c j i", i=4), w2_raw[:, :, cols].rearrange("p j (c i) -> p c j i", i=4))
+        def round_pair(pair, first_plane, n, copy):
+            start, width = PIECES[n]
+            copy(z_bf[n][:, :, first_plane : first_plane + 2], pair[:].rearrange("p (i s) -> p s i", i=2)[:, start : start + width, :])
 
-        m1 = [None] * PACK
-        ms = [sb("ms_%d" % t, [P, V], F32) for t in range(PACK)]
-        md = [sb("md_%d" % t, [P, V], F32) for t in range(PACK)]
-        early = sb("early", [P, 2 * S], F32)
-        pair = sb("pair", [P, 2 * S], F32, tag="early")
-        zb = [at("zb%d" % c, [P, width, PACK], BF16, 2 * PACK * start) for c, (start, width) in enumerate(CHUNKS)]
-
-        def fetch1(t):
-            if t in ORDER[1:3]:
-                m1[t] = at("m1_%d" % t, [P, V + 32], F32, 960)[:, 0:V]
-            else:
-                m1[t] = sb("m1_%d" % t, [P, V], F32, tag={ORDER[3]: "ms_%d" % ORDER[1]}.get(t))[:]
-            nc.vector.tensor_copy(m1[t], state[t][:].indirect(s1_t[:]))
+        def fetch1(t, after=None):
+            moved[t] = sbuf("moved%d" % t, [P, V], F32, after=after)
+            nc.vector.tensor_copy(moved[t][:], plane[t][:].indirect(s1_t[:]))
 
         def put1(t):
-            nc.vector.tensor_copy(state[t][:].indirect(d1_t[:]), m1[t])
-            if t == 2:
-                nc.scalar.activation(pair[:, 0:S], state[t][:], COPY, scale=2.0)
+            nc.vector.tensor_copy(plane[t][:].indirect(d1_t[:]), moved[t][:])
 
         def fetch2(t):
-            if t != 2:
-                nc.vector.tensor_scalar(ms[t][:], state[t][:].indirect(s2_t[:]), 0.5, 0.0, op0=MULT, op1=ADD)
-                nc.vector.tensor_scalar(md[t][:], state[t][:].indirect(d2_t[:]), 0.5, 0.0, op0=MULT, op1=ADD)
-            else:
-                nc.vector.tensor_copy(ms[t][:], state[t][:].indirect(s2_t[:]))
-                nc.vector.tensor_copy(md[t][:], state[t][:].indirect(d2_t[:]))
+            nc.vector.tensor_scalar(half_s[t][:], plane[t][:].indirect(s2_t[:]), 0.5, 0.0, op0=MULT, op1=ADD)
+            nc.vector.tensor_scalar(half_d[t][:], plane[t][:].indirect(d2_t[:]), 0.5, 0.0, op0=MULT, op1=ADD)
 
-        def put2(t):
-            window = pair if t == 2 else state[t]
-            nc.vector.tensor_tensor(window[:].indirect(d2_t[:]), ms[t][:], md[t][:], ADD)
-            if t < 2:
-                nc.scalar.copy(early[:, S * t : S * (t + 1)], state[t][:])
-            if t == 1:
-                early_v = early[:].rearrange("p (s j) -> p j s", s=2)
-                for c, (start, width) in enumerate(CHUNKS):
-                    nc.scalar.copy(zb[c][:, :, 0:2], early_v[:, start : start + width, :])
-            if t == 3:
-                nc.scalar.copy(pair[:, S : 2 * S], state[t][:])
+        def put2(t, window):
+            nc.vector.tensor_tensor(window[:].indirect(d2_t[:]), half_s[t][:], half_d[t][:], ADD)
 
-        a, b, c, d = ORDER
-        fetch1(a)
-        fetch1(b)
-        put1(a)
-        put1(b)
-        fetch2(a)
-        fetch2(b)
-        put2(a)
-        fetch1(c)
-        put2(b)
-        put1(c)
-        fetch1(d)
-        fetch2(c)
-        put1(d)
-        put2(c)
-        fetch2(d)
-        w2_c = [None] * len(CHUNKS)
-        w2_e = [sb("w2_e%d" % u, [P, width], U8) for u, (start, width) in enumerate(CHUNKS)]
+        fetch1(0)
+        fetch1(1)
+        put1(0)
+        put1(1)
+        fetch2(0)
+        fetch2(1)
+        put2(0, plane[0])
+        nc.scalar.copy(pair01[:, 0:S], plane[0][:])
+        fetch1(3, after="moved1")
+        put2(1, plane[1])
+        nc.scalar.copy(pair01[:, S : 2 * S], plane[1][:])
+        for n in range(len(PIECES)):
+            round_pair(pair01, 0, n, nc.scalar.copy)
+        put1(3)
+        fetch1(2, after="half_s1")
+        fetch2(3)
+        put1(2)
+        nc.scalar.copy(pair23[:, 0:S], plane[2][:])
+        put2(3, plane[3])
+        nc.scalar.copy(pair23[:, S : 2 * S], plane[3][:])
+        fetch2(2)
 
-        def w2_quant(u, codes):
-            w2_c[u] = codes
-            nc.vector.quantize_mx(out=codes[:].bitcast(FP8X4), scales=w2_e[u][:], in_=w2_g[u][:].rearrange("p c j -> p (c j)"))
+        w2_codes = [None] * len(PIECES)
+        w2_scales = [sbuf("w2_scales%d" % n, [P, width], U8) for n, (start, width) in enumerate(PIECES)]
 
-        w2_quant(0, sb("w2_c0", [P, P], U32, tag="ms_%d" % c))
-        for n in range(2):
-            warm = psum.tile([P, S], F32, name="acc")
-            nc.tensor.matmul_mx(out=warm[:], lhsT=w2_c[0][:].bitcast(FP8X4), lhsT_scale=w2_e[0][:], rhs=xg_all[:].bitcast(FP8X4), rhs_scale=xg_s[:], start=True, stop=True)
-        put2(d)
+        def quantise_w2(n, after):
+            w2_codes[n] = sbuf("w2_codes%d" % n, [P, PIECES[n][1]], U32, after=after)
+            quantise(w2_codes[n][:], w2_scales[n][:], w2_bf[n][:].rearrange("p c j -> p (c j)"))
 
-        pair_v = pair[:].rearrange("p (s j) -> p j s", s=2)
-        z_c = [sb("z_c%d" % h, [P, HALF], U32) for h in range(2)]
-        z_e = [sb("z_e%d" % h, [P, HALF], U8) for h in range(2)]
+        quantise_w2(0, after="half_s3")
+        for repeat in range(2):
+            product(w2_codes[0][:], w2_scales[0][:], x_words_picked[:], x_scales_picked[:], S)
+        put2(2, pair23)
 
-        def z_round(c, copy):
-            start, width = CHUNKS[c]
-            copy(zb[c][:, :, 2:4], pair_v[:, start : start + width, :])
+        z_codes = [sbuf("z_codes%d" % h, [P, HALF], U32) for h in range(2)]
+        z_scales = [sbuf("z_scales%d" % h, [P, HALF], U8) for h in range(2)]
 
-        def z_quant(c):
-            start, width = CHUNKS[c]
-            cols = slice(start % HALF, start % HALF + width)
-            nc.vector.quantize_mx(out=z_c[start // HALF][:, cols].bitcast(FP8X4), scales=z_e[start // HALF][:, cols], in_=zb[c][:].rearrange("p n j -> p (n j)"))
+        def quantise_z(n):
+            start, width = PIECES[n]
+            places = slice(start % HALF, start % HALF + width)
+            quantise(z_codes[start // HALF][:, places], z_scales[start // HALF][:, places], z_bf[n][:].rearrange("p s j -> p (s j)"))
 
-        z_round(0, nc.vector.tensor_copy)
-        z_round(1, nc.vector.tensor_copy)
-        z_round(2, nc.scalar.copy)
-        w2_quant(1, sb("w2_c1", [P, P], U32, tag="state%d" % c))
-        z_quant(0)
-        z_quant(1)
-        w2_quant(2, at("w2_c2", [P, HALF], U32, 0))
-        z_quant(2)
+        round_pair(pair23, 2, 0, nc.vector.tensor_copy)
+        round_pair(pair23, 2, 1, nc.vector.tensor_copy)
+        round_pair(pair23, 2, 2, nc.scalar.copy)
+        quantise_w2(1, after="plane3")
+        quantise_z(0)
+        quantise_z(1)
+        quantise_w2(2, after="z_bf0")
+        quantise_z(2)
 
-        out_v = out.rearrange("(b p) j -> p b j", p=P)
+        out_v = out.rearrange("(b p) s -> p b s", p=P)
 
-        def piece(b, start, width, copy, res):
-            u = min(b, 2)
-            rows = slice(P * (b - u), P * (b - u + 1))
-            cols = slice(start % HALF, start % HALF + width)
-            acc = psum.tile([P, width], F32, name="acc")
-            nc.tensor.matmul_mx(out=acc[:], lhsT=w2_c[u][:, rows].bitcast(FP8X4), lhsT_scale=w2_e[u][:, rows], rhs=z_c[start // HALF][:, cols].bitcast(FP8X4), rhs_scale=z_e[start // HALF][:, cols], start=True, stop=True)
-            copy(res, acc[:])
+        def result(b, start, width, copy, staged):
+            n = min(b, len(PIECES) - 1)
+            columns = slice(P * b - PIECES[n][0], P * (b + 1) - PIECES[n][0])
+            places = slice(start % HALF, start % HALF + width)
+            acc = product(w2_codes[n][:, columns], w2_scales[n][:, columns], z_codes[start // HALF][:, places], z_scales[start // HALF][:, places], width)
+            copy(staged, acc[:])
 
         def stored(b, start, width, copy):
-            res = sb("res%d_%d" % (b, start), [P, width], F32)
-            piece(b, start, width, copy, res[:])
-            nc.sync.dma_start(out_v[:, b, start : start + width], res[:])
+            staged = sbuf("staged%d_%d" % (b, start), [P, width], F32)
+            result(b, start, width, copy, staged[:])
+            nc.sync.dma_start(out_v[:, b, start : start + width], staged[:])
 
         stored(0, 0, P, nc.scalar.copy)
-        second = sb("res_second", [P, HALF], F32)
-        piece(1, 0, P, nc.scalar.copy, second[:, 0:P])
+        staged_1 = sbuf("staged_1", [P, HALF], F32)
+        result(1, 0, P, nc.scalar.copy, staged_1[:, 0:P])
         stored(0, P, P, nc.scalar.copy)
-        piece(1, P, P, nc.scalar.copy, second[:, P:HALF])
-        nc.sync.dma_start(out_v[:, 1, 0:HALF], second[:])
-        for b in range(2, PACK):
-            stored(b, 0, HALF, nc.scalar.copy if b < 3 else nc.vector.tensor_copy)
-        for b in range(PACK - 1):
-            stored(b, HALF, HALF, nc.vector.tensor_copy if b % 2 else nc.scalar.copy)
-        last = sb("res_last", [P, HALF], F32)
-        piece(PACK - 1, HALF, P, nc.vector.tensor_copy, last[:, 0:P])
-        piece(PACK - 1, HALF + P, P, nc.vector.tensor_copy, last[:, P:HALF])
-        nc.sync.dma_start(out_v[:, PACK - 1, HALF:S], last[:])
+        result(1, P, P, nc.scalar.copy, staged_1[:, P:HALF])
+        nc.sync.dma_start(out_v[:, 1, 0:HALF], staged_1[:])
+        stored(2, 0, HALF, nc.scalar.copy)
+        stored(3, 0, HALF, nc.vector.tensor_copy)
+        stored(0, HALF, HALF, nc.scalar.copy)
+        stored(1, HALF, HALF, nc.vector.tensor_copy)
+        stored(2, HALF, HALF, nc.scalar.copy)
+        staged_last = sbuf("staged_last", [P, HALF], F32)
+        result(3, HALF, P, nc.vector.tensor_copy, staged_last[:, 0:P])
+        result(3, HALF + P, P, nc.vector.tensor_copy, staged_last[:, P:HALF])
+        nc.sync.dma_start(out_v[:, 3, HALF:S], staged_last[:])

@@ -12,6 +12,7 @@ U32 = mybir.dt.uint32
 U16 = mybir.dt.uint16
 U8 = mybir.dt.uint8
 FP8X4 = mybir.dt.float8_e4m3fn_x4
+COPY = mybir.ActivationFunctionType.Copy
 MULT = mybir.AluOpType.mult
 ADD = mybir.AluOpType.add
 
@@ -61,34 +62,34 @@ def tile_picked_carry2_none_p_kernel(tc, x_words, x_scales, w1, w2, offs, s1, d1
         for tile, src in ((s1_t, s1), (d1_t, d1), (s2_t, s2), (d2_t, d2)):
             nc.sync.dma_start(tile[:], src)
 
-        w1_bf = [sbuf("w1_bf%d" % u, [P, 2, P, PACK], BF16) for u in range(2)]
-        w1_codes = [sbuf("w1_codes%d" % u, [P, 2 * P], U32) for u in range(2)]
-        w1_scales = [sbuf("w1_scales%d" % u, [P, 2 * P], U8) for u in range(2)]
+        w1_bf = [sbuf("w1_bf%d" % g, [P, 2, P, PACK], BF16) for g in range(2)]
+        w1_codes = [sbuf("w1_codes%d" % g, [P, 2 * P], U32) for g in range(2)]
+        w1_scales = [sbuf("w1_scales%d" % g, [P, 2 * P], U8) for g in range(2)]
 
-        def lay_w1(u, e, copy):
-            src = w1_raw[e][:].rearrange("p j (m t) -> p m j t", t=PACK)[:, :, :, 2 * u : 2 * u + 2]
-            copy(w1_bf[u][:, :, :, 2 * e : 2 * e + 2].rearrange("p i m j -> p m j i"), src)
+        def lay_w1(g, e, copy):
+            src = w1_raw[e][:].rearrange("p j (m t) -> p m j t", t=PACK)[:, :, :, 2 * g : 2 * g + 2]
+            copy(w1_bf[g][:, :, :, 2 * e : 2 * e + 2].rearrange("p i m j -> p m j i"), src)
 
         x_scales_spread = sbuf("x_scales_spread", [P, S], U8)
         x_scales_picked = sbuf("x_scales_picked", [P, S], U8)
         x_words_picked = sbuf("x_words_picked", [P, S], U32)
 
-        lay_w1(0, 0, nc.scalar.copy)
         lay_w1(1, 0, nc.scalar.copy)
+        lay_w1(0, 0, nc.scalar.copy)
         nc.vector.tensor_copy(x_scales_spread[:], x_scale_rows[:].indirect(offs_t[:]))
         nc.vector.tensor_copy(x_scales_picked[:].bitcast(I32), x_scales_spread[:].bitcast(I32))
         for r in range(1, 4):
             nc.scalar.dma_start(x_scales_picked[r:P:QUADRANT, :].bitcast(I32), x_scales_spread[SPREAD * r : P : QUADRANT, :].bitcast(I32))
-        lay_w1(0, 1, nc.vector.tensor_copy)
-        lay_w1(1, 1, nc.scalar.copy)
+        lay_w1(1, 1, nc.vector.tensor_copy)
+        lay_w1(0, 1, nc.scalar.copy)
         w2_raw = sbuf("w2_raw", [P, PACK, N], F32, after="x_scales_spread")
         nc.sync.dma_start(w2_raw[:], w2.rearrange("(p j) c -> p j c", j=PACK))
-        for u in range(2):
-            quantise(w1_codes[u][:], w1_scales[u][:], w1_bf[u][:].rearrange("p i m j -> p (i m j)"))
+        for g in (1, 0):
+            quantise(w1_codes[g][:], w1_scales[g][:], w1_bf[g][:].rearrange("p i m j -> p (i m j)"))
         for start in (0, HALF):
             nc.vector.tensor_copy(x_words_picked[:, start : start + HALF], x_word_rows[:].indirect(offs_t[:, start // 16 : (start + HALF) // 16]))
 
-        plane = [sbuf("plane%d" % t, [P, S], F32) for t in range(PACK)]
+        plane = [sbuf("plane%d" % t, [P, 2 * S if t < 2 else S], F32) for t in range(PACK)]
 
         def project(t, start, width, copy):
             places = slice(start, start + width)
@@ -96,79 +97,65 @@ def tile_picked_carry2_none_p_kernel(tc, x_words, x_scales, w1, w2, offs, s1, d1
             acc = product(w1_codes[t // 2][:, columns], w1_scales[t // 2][:, columns], x_words_picked[:, places], x_scales_picked[:, places], width)
             copy(plane[t][:, places], acc[:])
 
-        project(0, 0, HALF, nc.scalar.copy)
-        project(1, 0, HALF, nc.vector.tensor_copy)
-        project(0, HALF, P, nc.vector.tensor_copy)
-        project(0, HALF + P, P, nc.scalar.copy)
-        project(1, HALF, HALF, nc.scalar.copy)
-        for t in (3, 2):
-            for start in (0, HALF):
-                project(t, start, HALF, nc.scalar.copy)
-
-        w2_bf = [sbuf("w2_bf%d" % n, [P, width, PACK], BF16) for n, (start, width) in enumerate(PIECES)]
-        for n, (start, width) in enumerate(PIECES):
-            for first in range(0, width, P):
-                src = w2_raw[:, :, start + first : start + first + P]
-                nc.scalar.copy(w2_bf[n][:, first : first + P, :].rearrange("p (c i) j -> p c j i", i=4), src.rearrange("p j (c i) -> p c j i", i=4))
-
-        moved = [None] * PACK
+        moved = [sbuf("moved%d" % t, [P, V], F32) for t in range(PACK)]
         half_s = [sbuf("half_s%d" % t, [P, V], F32) for t in range(PACK)]
         half_d = [sbuf("half_d%d" % t, [P, V], F32) for t in range(PACK)]
-        pair01 = sbuf("pair01", [P, 2 * S], F32)
-        pair23 = sbuf("pair23", [P, 2 * S], F32, after="pair01")
         z_bf = [sbuf("z_bf%d" % n, [P, width, PACK], BF16) for n, (start, width) in enumerate(PIECES)]
 
-        def round_pair(pair, first_plane, n, copy):
+        def round_pair(u, n, copy):
             start, width = PIECES[n]
-            copy(z_bf[n][:, :, first_plane : first_plane + 2], pair[:].rearrange("p (i s) -> p s i", i=2)[:, start : start + width, :])
+            copy(z_bf[n][:, :, 2 * u : 2 * u + 2], plane[u][:].rearrange("p (i s) -> p s i", i=2)[:, start : start + width, :])
 
-        def fetch1(t, after=None):
-            moved[t] = sbuf("moved%d" % t, [P, V], F32, after=after)
-            nc.vector.tensor_copy(moved[t][:], plane[t][:].indirect(s1_t[:]))
-
-        def put1(t):
+        def round1(t):
+            nc.scalar.activation(moved[t][:], plane[t][:].indirect(s1_t[:]), COPY)
             nc.vector.tensor_copy(plane[t][:].indirect(d1_t[:]), moved[t][:])
 
         def fetch2(t):
-            nc.vector.tensor_scalar(half_s[t][:], plane[t][:].indirect(s2_t[:]), 0.5, 0.0, op0=MULT, op1=ADD)
-            nc.vector.tensor_scalar(half_d[t][:], plane[t][:].indirect(d2_t[:]), 0.5, 0.0, op0=MULT, op1=ADD)
+            nc.scalar.activation(half_s[t][:], plane[t][:].indirect(s2_t[:]), COPY, scale=0.5)
+            nc.scalar.activation(half_d[t][:], plane[t][:].indirect(d2_t[:]), COPY, scale=0.5)
 
-        def put2(t, window):
-            nc.vector.tensor_tensor(window[:].indirect(d2_t[:]), half_s[t][:], half_d[t][:], ADD)
+        def put2(t):
+            nc.vector.tensor_tensor(plane[t][:].indirect(d2_t[:]), half_s[t][:], half_d[t][:], ADD)
 
-        fetch1(0)
-        fetch1(1)
-        put1(0)
-        put1(1)
-        fetch2(0)
-        fetch2(1)
-        put2(0, plane[0])
-        nc.scalar.copy(pair01[:, 0:S], plane[0][:])
-        fetch1(3, after="moved1")
-        put2(1, plane[1])
-        nc.scalar.copy(pair01[:, S : 2 * S], plane[1][:])
-        for n in range(len(PIECES)):
-            round_pair(pair01, 0, n, nc.scalar.copy)
-        put1(3)
-        fetch1(2, after="half_s1")
-        fetch2(3)
-        put1(2)
-        nc.scalar.copy(pair23[:, 0:S], plane[2][:])
-        put2(3, plane[3])
-        nc.scalar.copy(pair23[:, S : 2 * S], plane[3][:])
+        def join(u):
+            nc.scalar.copy(plane[u][:, S : 2 * S], plane[2 + u][:])
+
+        project(2, 0, HALF, nc.scalar.copy)
+        project(3, 0, HALF, nc.vector.tensor_copy)
+        project(2, HALF, P, nc.vector.tensor_copy)
+        project(2, HALF + P, P, nc.scalar.copy)
+        project(3, HALF, HALF, nc.vector.tensor_copy)
+        round1(2)
+        round1(3)
+        project(0, 0, S, nc.scalar.copy)
+
+        w2_bf = [sbuf("w2_bf%d" % h, [P, HALF, PACK], BF16) for h in range(2)]
+        for h in range(2):
+            src = w2_raw[:, :, HALF * h : HALF * (h + 1)].rearrange("p (i u) c -> p c u i", i=2)
+            nc.gpsimd.tensor_scalar(w2_bf[h][:].rearrange("p c (u i) -> p c u i", i=2), src, 1.0, 0.0, op0=MULT, op1=ADD)
+
+        round1(0)
         fetch2(2)
+        put2(2)
+        project(1, 0, S, nc.scalar.copy)
+        round1(1)
+        fetch2(3)
+        put2(3)
+        fetch2(0)
+        join(0)
+        put2(0)
+        fetch2(1)
+        join(1)
+        put2(1)
+        for n in range(len(PIECES)):
+            round_pair(0, n, nc.scalar.copy)
 
-        w2_codes = [None] * len(PIECES)
-        w2_scales = [sbuf("w2_scales%d" % n, [P, width], U8) for n, (start, width) in enumerate(PIECES)]
+        w2_codes = [None] * 2
+        w2_scales = [sbuf("w2_scales%d" % h, [P, HALF], U8) for h in range(2)]
 
-        def quantise_w2(n, after):
-            w2_codes[n] = sbuf("w2_codes%d" % n, [P, PIECES[n][1]], U32, after=after)
-            quantise(w2_codes[n][:], w2_scales[n][:], w2_bf[n][:].rearrange("p c j -> p (c j)"))
-
-        quantise_w2(0, after="half_s3")
-        for repeat in range(2):
-            product(w2_codes[0][:], w2_scales[0][:], x_words_picked[:], x_scales_picked[:], S)
-        put2(2, pair23)
+        def quantise_w2(h, after):
+            w2_codes[h] = sbuf("w2_codes%d" % h, [P, HALF], U32, after=after)
+            quantise(w2_codes[h][:], w2_scales[h][:], w2_bf[h][:].rearrange("p c j -> p (c j)"))
 
         z_codes = [sbuf("z_codes%d" % h, [P, HALF], U32) for h in range(2)]
         z_scales = [sbuf("z_scales%d" % h, [P, HALF], U8) for h in range(2)]
@@ -178,22 +165,21 @@ def tile_picked_carry2_none_p_kernel(tc, x_words, x_scales, w1, w2, offs, s1, d1
             places = slice(start % HALF, start % HALF + width)
             quantise(z_codes[start // HALF][:, places], z_scales[start // HALF][:, places], z_bf[n][:].rearrange("p s j -> p (s j)"))
 
-        round_pair(pair23, 2, 0, nc.vector.tensor_copy)
-        round_pair(pair23, 2, 1, nc.vector.tensor_copy)
-        round_pair(pair23, 2, 2, nc.scalar.copy)
-        quantise_w2(1, after="plane3")
+        quantise_w2(0, after="plane3")
+        round_pair(1, 0, nc.vector.tensor_copy)
+        round_pair(1, 1, nc.vector.tensor_copy)
+        round_pair(1, 2, nc.scalar.copy)
         quantise_z(0)
         quantise_z(1)
-        quantise_w2(2, after="z_bf0")
+        quantise_w2(1, after="z_bf0")
         quantise_z(2)
 
         out_v = out.rearrange("(b p) s -> p b s", p=P)
 
         def result(b, start, width, copy, staged):
-            n = min(b, len(PIECES) - 1)
-            columns = slice(P * b - PIECES[n][0], P * (b + 1) - PIECES[n][0])
+            columns = slice(P * (b % 2), P * (b % 2 + 1))
             places = slice(start % HALF, start % HALF + width)
-            acc = product(w2_codes[n][:, columns], w2_scales[n][:, columns], z_codes[start // HALF][:, places], z_scales[start // HALF][:, places], width)
+            acc = product(w2_codes[b // 2][:, columns], w2_scales[b // 2][:, columns], z_codes[start // HALF][:, places], z_scales[start // HALF][:, places], width)
             copy(staged, acc[:])
 
         def stored(b, start, width, copy):

@@ -29,7 +29,7 @@ def tile_picked_carry2_none_p_kernel(tc, x_words, x_scales, w1, w2, offs, s1, d1
     with ExitStack() as ctx:
         lists = ctx.enter_context(tc.tile_pool(name="lists", bufs=1))
         keep = ctx.enter_context(tc.tile_pool(name="keep", bufs=1))
-        psum = ctx.enter_context(tc.psum_pool(name="psum", bufs=8))
+        psum = ctx.enter_context(tc.psum_pool(name="psum", bufs=1))
 
         def sbuf(name, shape, dtype, after=None):
             return keep.tile(shape, dtype, name=name, tag=after or name, align_bytes=64)
@@ -37,10 +37,11 @@ def tile_picked_carry2_none_p_kernel(tc, x_words, x_scales, w1, w2, offs, s1, d1
         def quantise(codes, scales, values):
             nc.vector.quantize_mx(out=codes.bitcast(FP8X4), scales=scales, in_=values)
 
-        def product(codes_l, scales_l, codes_r, scales_r, width):
-            acc = psum.tile([P, width], F32, name="acc")
-            nc.tensor.matmul_mx(out=acc[:], lhsT=codes_l.bitcast(FP8X4), lhsT_scale=scales_l, rhs=codes_r.bitcast(FP8X4), rhs_scale=scales_r, start=True, stop=True)
-            return acc
+        def banks(n, width):
+            return psum.tile([P, width], F32, name="acc", tag="banks%d" % n)
+
+        def product(acc, codes_l, scales_l, codes_r, scales_r):
+            nc.tensor.matmul_mx(out=acc, lhsT=codes_l.bitcast(FP8X4), lhsT_scale=scales_l, rhs=codes_r.bitcast(FP8X4), rhs_scale=scales_r, start=True, stop=True)
 
         offs_t = lists.tile([P, S // 16], U16, name="offs_t")
         s1_t = lists.tile([P, V // 16], U16, name="s1_t")
@@ -86,16 +87,16 @@ def tile_picked_carry2_none_p_kernel(tc, x_words, x_scales, w1, w2, offs, s1, d1
         nc.sync.dma_start(w2_raw[:], w2.rearrange("(p j) c -> p j c", j=PACK))
         for g in (1, 0):
             quantise(w1_codes[g][:], w1_scales[g][:], w1_bf[g][:].rearrange("p i m j -> p (i m j)"))
-        for start in (0, HALF):
-            nc.vector.tensor_copy(x_words_picked[:, start : start + HALF], x_word_rows[:].indirect(offs_t[:, start // 16 : (start + HALF) // 16]))
+        for start, width in ((0, HALF), (HALF, P), (HALF + P, P)):
+            nc.vector.tensor_copy(x_words_picked[:, start : start + width], x_word_rows[:].indirect(offs_t[:, start // 16 : (start + width) // 16]))
 
         plane = [sbuf("plane%d" % t, [P, 2 * S if t < 2 else S], F32) for t in range(PACK)]
 
-        def project(t, start, width, copy):
+        def project(t, start, width, copy, acc):
             places = slice(start, start + width)
             columns = slice(P * (t % 2), P * (t % 2 + 1))
-            acc = product(w1_codes[t // 2][:, columns], w1_scales[t // 2][:, columns], x_words_picked[:, places], x_scales_picked[:, places], width)
-            copy(plane[t][:, places], acc[:])
+            product(acc, w1_codes[t // 2][:, columns], w1_scales[t // 2][:, columns], x_words_picked[:, places], x_scales_picked[:, places])
+            copy(plane[t][:, places], acc)
 
         moved = [sbuf("moved%d" % t, [P, V], F32) for t in range(PACK)]
         half_s = [sbuf("half_s%d" % t, [P, V], F32) for t in range(PACK)]
@@ -120,14 +121,16 @@ def tile_picked_carry2_none_p_kernel(tc, x_words, x_scales, w1, w2, offs, s1, d1
         def join(u):
             nc.scalar.copy(plane[u][:, S : 2 * S], plane[2 + u][:])
 
-        project(2, 0, HALF, nc.scalar.copy)
-        project(3, 0, HALF, nc.vector.tensor_copy)
-        project(2, HALF, P, nc.vector.tensor_copy)
-        project(2, HALF + P, P, nc.scalar.copy)
-        project(3, HALF, HALF, nc.vector.tensor_copy)
+        project(2, 0, HALF, nc.scalar.copy, banks(0, HALF)[:])
+        project(2, HALF, P, nc.scalar.copy, banks(2, P)[:])
+        project(2, HALF + P, P, nc.vector.tensor_copy, banks(3, P)[:])
+        project(3, 0, HALF, nc.vector.tensor_copy, banks(0, HALF)[:])
+        project(3, HALF, HALF, nc.vector.tensor_copy, banks(4, HALF)[:])
         round1(2)
         round1(3)
-        project(0, 0, S, nc.scalar.copy)
+        both = banks(4, 2 * S)
+        for t in range(2):
+            project(t, 0, S, nc.scalar.copy, both[:, S * t : S * (t + 1)])
 
         w2_bf = [sbuf("w2_bf%d" % h, [P, HALF, PACK], BF16) for h in range(2)]
         for h in range(2):
@@ -137,7 +140,6 @@ def tile_picked_carry2_none_p_kernel(tc, x_words, x_scales, w1, w2, offs, s1, d1
         round1(0)
         fetch2(2)
         put2(2)
-        project(1, 0, S, nc.scalar.copy)
         round1(1)
         fetch2(3)
         put2(3)
@@ -176,10 +178,14 @@ def tile_picked_carry2_none_p_kernel(tc, x_words, x_scales, w1, w2, offs, s1, d1
 
         out_v = out.rearrange("(b p) s -> p b s", p=P)
 
+        done = []
+
         def result(b, start, width, copy, staged):
             columns = slice(P * (b % 2), P * (b % 2 + 1))
             places = slice(start % HALF, start % HALF + width)
-            acc = product(w2_codes[b // 2][:, columns], w2_scales[b // 2][:, columns], z_codes[start // HALF][:, places], z_scales[start // HALF][:, places], width)
+            done.append(b)
+            acc = banks(len(done) % 7, width)
+            product(acc[:], w2_codes[b // 2][:, columns], w2_scales[b // 2][:, columns], z_codes[start // HALF][:, places], z_scales[start // HALF][:, places])
             copy(staged, acc[:])
 
         def stored(b, start, width, copy):

@@ -37,8 +37,11 @@ def tile_picked_carry2_none_p_kernel(tc, x_words, x_scales, w1, w2, offs, s1, d1
         def quantise(codes, scales, values):
             nc.vector.quantize_mx(out=codes.bitcast(FP8X4), scales=scales, in_=values)
 
+        made = []
+
         def banks(n, width):
-            return psum.tile([P, width], F32, name="acc", tag="banks%d" % n)
+            made.append(n)
+            return psum.tile([P, width], F32, name="acc%d" % len(made), offset=2048 * n)
 
         def product(acc, codes_l, scales_l, codes_r, scales_r):
             nc.tensor.matmul_mx(out=acc, lhsT=codes_l.bitcast(FP8X4), lhsT_scale=scales_l, rhs=codes_r.bitcast(FP8X4), rhs_scale=scales_r, start=True, stop=True)
@@ -125,12 +128,11 @@ def tile_picked_carry2_none_p_kernel(tc, x_words, x_scales, w1, w2, offs, s1, d1
         project(2, HALF, P, nc.scalar.copy, banks(2, P)[:])
         project(2, HALF + P, P, nc.vector.tensor_copy, banks(3, P)[:])
         project(3, 0, HALF, nc.vector.tensor_copy, banks(0, HALF)[:])
-        project(3, HALF, HALF, nc.vector.tensor_copy, banks(4, HALF)[:])
+        project(3, HALF, HALF, nc.vector.tensor_copy, banks(4, 2 * S)[:, 0:HALF])
         round1(2)
         round1(3)
-        both = banks(4, 2 * S)
         for t in range(2):
-            project(t, 0, S, nc.scalar.copy, both[:, S * t : S * (t + 1)])
+            project(t, 0, S, nc.scalar.copy, banks(4 + t, S)[:])
 
         w2_bf = [sbuf("w2_bf%d" % h, [P, HALF, PACK], BF16) for h in range(2)]
         for h in range(2):
@@ -138,9 +140,9 @@ def tile_picked_carry2_none_p_kernel(tc, x_words, x_scales, w1, w2, offs, s1, d1
             nc.gpsimd.tensor_scalar(w2_bf[h][:].rearrange("p c (u i) -> p c u i", i=2), src, 1.0, 0.0, op0=MULT, op1=ADD)
 
         round1(0)
+        round1(1)
         fetch2(2)
         put2(2)
-        round1(1)
         fetch2(3)
         put2(3)
         fetch2(0)
@@ -184,7 +186,7 @@ def tile_picked_carry2_none_p_kernel(tc, x_words, x_scales, w1, w2, offs, s1, d1
             columns = slice(P * (b % 2), P * (b % 2 + 1))
             places = slice(start % HALF, start % HALF + width)
             done.append(b)
-            acc = banks(len(done) % 7, width)
+            acc = banks(len(done) % 8, width)
             product(acc[:], w2_codes[b // 2][:, columns], w2_scales[b // 2][:, columns], z_codes[start // HALF][:, places], z_scales[start // HALF][:, places])
             copy(staged, acc[:])
 

@@ -21,7 +21,9 @@ PACK = 4
 HALF = 256
 QUADRANT = 32
 SPREAD = 8
-PIECES = ((0, 128), (128, 128), (256, 256))
+BANKS, BANK_BYTES = 8, 2048
+X_PIECES = ((0, 256), (256, 128), (384, 128))
+Z_PIECES = ((0, 128), (128, 128), (256, 256))
 
 
 def tile_picked_carry2_none_p_kernel(tc, x_words, x_scales, w1, w2, offs, s1, d1, s2, d2, out):
@@ -34,14 +36,11 @@ def tile_picked_carry2_none_p_kernel(tc, x_words, x_scales, w1, w2, offs, s1, d1
         def sbuf(name, shape, dtype, after=None):
             return keep.tile(shape, dtype, name=name, tag=after or name, align_bytes=64)
 
+        def bank(name, number, width):
+            return psum.tile([P, width], F32, name=name, offset=BANK_BYTES * number)
+
         def quantise(codes, scales, values):
             nc.vector.quantize_mx(out=codes.bitcast(FP8X4), scales=scales, in_=values)
-
-        made = []
-
-        def banks(n, width):
-            made.append(n)
-            return psum.tile([P, width], F32, name="acc%d" % len(made), offset=2048 * n)
 
         def product(acc, codes_l, scales_l, codes_r, scales_r):
             nc.tensor.matmul_mx(out=acc, lhsT=codes_l.bitcast(FP8X4), lhsT_scale=scales_l, rhs=codes_r.bitcast(FP8X4), rhs_scale=scales_r, start=True, stop=True)
@@ -72,7 +71,7 @@ def tile_picked_carry2_none_p_kernel(tc, x_words, x_scales, w1, w2, offs, s1, d1
 
         def lay_w1(g, e, copy):
             src = w1_raw[e][:].rearrange("p j (m t) -> p m j t", t=PACK)[:, :, :, 2 * g : 2 * g + 2]
-            copy(w1_bf[g][:, :, :, 2 * e : 2 * e + 2].rearrange("p i m j -> p m j i"), src)
+            copy(w1_bf[g][:, :, :, 2 * e : 2 * e + 2].rearrange("p u m j -> p m j u"), src)
 
         x_scales_spread = sbuf("x_scales_spread", [P, S], U8)
         x_scales_picked = sbuf("x_scales_picked", [P, S], U8)
@@ -89,104 +88,93 @@ def tile_picked_carry2_none_p_kernel(tc, x_words, x_scales, w1, w2, offs, s1, d1
         w2_raw = sbuf("w2_raw", [P, PACK, N], F32, after="x_scales_spread")
         nc.sync.dma_start(w2_raw[:], w2.rearrange("(p j) c -> p j c", j=PACK))
         for g in (1, 0):
-            quantise(w1_codes[g][:], w1_scales[g][:], w1_bf[g][:].rearrange("p i m j -> p (i m j)"))
-        for start, width in ((0, HALF), (HALF, P), (HALF + P, P)):
+            quantise(w1_codes[g][:], w1_scales[g][:], w1_bf[g][:].rearrange("p u m j -> p (u m j)"))
+        for start, width in X_PIECES:
             nc.vector.tensor_copy(x_words_picked[:, start : start + width], x_word_rows[:].indirect(offs_t[:, start // 16 : (start + width) // 16]))
 
         plane = [sbuf("plane%d" % t, [P, 2 * S if t < 2 else S], F32) for t in range(PACK)]
-
-        def project(t, start, width, copy, acc):
-            places = slice(start, start + width)
-            columns = slice(P * (t % 2), P * (t % 2 + 1))
-            product(acc, w1_codes[t // 2][:, columns], w1_scales[t // 2][:, columns], x_words_picked[:, places], x_scales_picked[:, places])
-            copy(plane[t][:, places], acc)
-
         moved = [sbuf("moved%d" % t, [P, V], F32) for t in range(PACK)]
         half_s = [sbuf("half_s%d" % t, [P, V], F32) for t in range(PACK)]
         half_d = [sbuf("half_d%d" % t, [P, V], F32) for t in range(PACK)]
-        z_bf = [sbuf("z_bf%d" % n, [P, width, PACK], BF16) for n, (start, width) in enumerate(PIECES)]
+        z_bf = [sbuf("z_bf%d" % n, [P, width, PACK], BF16) for n, (start, width) in enumerate(Z_PIECES)]
 
-        def round_pair(u, n, copy):
-            start, width = PIECES[n]
-            copy(z_bf[n][:, :, 2 * u : 2 * u + 2], plane[u][:].rearrange("p (i s) -> p s i", i=2)[:, start : start + width, :])
+        def project(t, start, width, copy, first_bank, banks_taken=1):
+            places = slice(start, start + width)
+            columns = slice(P * (t % 2), P * (t % 2 + 1))
+            acc = bank("y%d_%d" % (t, start), first_bank, banks_taken * S)[:, 0:width]
+            product(acc, w1_codes[t // 2][:, columns], w1_scales[t // 2][:, columns], x_words_picked[:, places], x_scales_picked[:, places])
+            copy(plane[t][:, places], acc)
 
-        def round1(t):
+        def first_round(t):
             nc.scalar.activation(moved[t][:], plane[t][:].indirect(s1_t[:]), COPY)
             nc.vector.tensor_copy(plane[t][:].indirect(d1_t[:]), moved[t][:])
 
-        def fetch2(t):
+        def fetch_halves(t):
             nc.scalar.activation(half_s[t][:], plane[t][:].indirect(s2_t[:]), COPY, scale=0.5)
             nc.scalar.activation(half_d[t][:], plane[t][:].indirect(d2_t[:]), COPY, scale=0.5)
 
-        def put2(t):
+        def put_means(t):
             nc.vector.tensor_tensor(plane[t][:].indirect(d2_t[:]), half_s[t][:], half_d[t][:], ADD)
 
-        def join(u):
-            nc.scalar.copy(plane[u][:, S : 2 * S], plane[2 + u][:])
+        def round_pair(u, n, copy):
+            start, width = Z_PIECES[n]
+            copy(z_bf[n][:, :, 2 * u : 2 * u + 2], plane[u][:].rearrange("p (i s) -> p s i", i=2)[:, start : start + width, :])
 
-        project(2, 0, HALF, nc.scalar.copy, banks(0, HALF)[:])
-        project(2, HALF, P, nc.scalar.copy, banks(2, P)[:])
-        project(2, HALF + P, P, nc.vector.tensor_copy, banks(3, P)[:])
-        project(3, 0, HALF, nc.vector.tensor_copy, banks(0, HALF)[:])
-        project(3, HALF, HALF, nc.vector.tensor_copy, banks(4, 2 * S)[:, 0:HALF])
-        round1(2)
-        round1(3)
-        for t in range(2):
-            project(t, 0, S, nc.scalar.copy, banks(4 + t, S)[:])
+        for (start, width), copy, number in zip(X_PIECES, (nc.scalar.copy, nc.scalar.copy, nc.vector.tensor_copy), (0, 2, 3)):
+            project(2, start, width, copy, number)
+        project(3, 0, HALF, nc.vector.tensor_copy, 0)
+        first_round(2)
+        project(3, HALF, HALF, nc.scalar.copy, 4, banks_taken=2)
+        first_round(3)
+        for u in range(2):
+            project(u, 0, S, nc.scalar.copy, 4 + u)
 
         w2_bf = [sbuf("w2_bf%d" % h, [P, HALF, PACK], BF16) for h in range(2)]
         for h in range(2):
             src = w2_raw[:, :, HALF * h : HALF * (h + 1)].rearrange("p (i u) c -> p c u i", i=2)
             nc.gpsimd.tensor_scalar(w2_bf[h][:].rearrange("p c (u i) -> p c u i", i=2), src, 1.0, 0.0, op0=MULT, op1=ADD)
 
-        round1(0)
-        round1(1)
-        fetch2(2)
-        put2(2)
-        fetch2(3)
-        put2(3)
-        fetch2(0)
-        join(0)
-        put2(0)
-        fetch2(1)
-        join(1)
-        put2(1)
-        for n in range(len(PIECES)):
+        for u in range(2):
+            first_round(u)
+        for u in range(2):
+            fetch_halves(2 + u)
+            put_means(2 + u)
+        for u in range(2):
+            fetch_halves(u)
+            nc.scalar.copy(plane[u][:, S : 2 * S], plane[2 + u][:])
+            put_means(u)
+        for n in range(len(Z_PIECES)):
             round_pair(0, n, nc.scalar.copy)
 
-        w2_codes = [None] * 2
+        w2_codes = [sbuf("w2_codes%d" % h, [P, HALF], U32, after=after) for h, after in enumerate(("plane3", "z_bf0"))]
         w2_scales = [sbuf("w2_scales%d" % h, [P, HALF], U8) for h in range(2)]
-
-        def quantise_w2(h, after):
-            w2_codes[h] = sbuf("w2_codes%d" % h, [P, HALF], U32, after=after)
-            quantise(w2_codes[h][:], w2_scales[h][:], w2_bf[h][:].rearrange("p c j -> p (c j)"))
-
         z_codes = [sbuf("z_codes%d" % h, [P, HALF], U32) for h in range(2)]
         z_scales = [sbuf("z_scales%d" % h, [P, HALF], U8) for h in range(2)]
 
+        def quantise_w2(h):
+            quantise(w2_codes[h][:], w2_scales[h][:], w2_bf[h][:].rearrange("p c j -> p (c j)"))
+
         def quantise_z(n):
-            start, width = PIECES[n]
+            start, width = Z_PIECES[n]
             places = slice(start % HALF, start % HALF + width)
             quantise(z_codes[start // HALF][:, places], z_scales[start // HALF][:, places], z_bf[n][:].rearrange("p s j -> p (s j)"))
 
-        quantise_w2(0, after="plane3")
+        quantise_w2(0)
         round_pair(1, 0, nc.vector.tensor_copy)
         round_pair(1, 1, nc.vector.tensor_copy)
         round_pair(1, 2, nc.scalar.copy)
         quantise_z(0)
         quantise_z(1)
-        quantise_w2(1, after="z_bf0")
+        quantise_w2(1)
         quantise_z(2)
 
         out_v = out.rearrange("(b p) s -> p b s", p=P)
-
-        done = []
+        banks_in_turn = [n % BANKS for n in range(11, 0, -1)]
 
         def result(b, start, width, copy, staged):
             columns = slice(P * (b % 2), P * (b % 2 + 1))
             places = slice(start % HALF, start % HALF + width)
-            done.append(b)
-            acc = banks(len(done) % 8, width)
+            acc = bank("out%d_%d" % (b, start), banks_in_turn.pop(), width)
             product(acc[:], w2_codes[b // 2][:, columns], w2_scales[b // 2][:, columns], z_codes[start // HALF][:, places], z_scales[start // HALF][:, places])
             copy(staged, acc[:])
 

@@ -106,7 +106,11 @@ def tile_picked_carry2_none_p_kernel(tc, x_words, x_scales, w1, w2, offs, s1, d1
             copy(plane[t][:, places], acc)
 
         def first_round(t):
-            nc.scalar.activation(moved[t][:], plane[t][:].indirect(s1_t[:]), COPY)
+            if t == 2:
+                nc.vector.tensor_copy(moved[t][:, 0:P], plane[t][:].indirect(s1_t[:, 0 : P // 16]))
+                nc.scalar.activation(moved[t][:, P:V], plane[t][:].indirect(s1_t[:, P // 16 : V // 16]), COPY)
+            else:
+                nc.scalar.activation(moved[t][:], plane[t][:].indirect(s1_t[:]), COPY)
             nc.vector.tensor_copy(plane[t][:].indirect(d1_t[:]), moved[t][:])
 
         def fetch_halves(t):

@@ -128,10 +128,11 @@ def tile_picked_carry2_none_p_kernel(tc, x_words, x_scales, w1, w2, offs, s1, d1
             project(2, start, width, copy, number)
         project(3, 0, HALF, nc.vector.tensor_copy, 0)
         first_round(2)
-        project(3, HALF, HALF, nc.scalar.copy, 4, banks_taken=2)
+        project(3, HALF, HALF, nc.scalar.copy, 4, banks_taken=3)
         first_round(3)
-        for u in range(2):
-            project(u, 0, S, nc.scalar.copy, 4 + u)
+        project(0, 0, HALF, nc.scalar.copy, 4)
+        project(0, HALF, HALF, nc.scalar.copy, 5)
+        project(1, 0, S, nc.scalar.copy, 6)
 
         w2_bf = [sbuf("w2_bf%d" % h, [P, HALF, PACK], BF16) for h in range(2)]
         for h in range(2):

@@ -84,7 +84,7 @@ def tile_picked_carry2_none_p_kernel(tc, x_words, x_scales, w1, w2, offs, s1, d1
         for r in range(1, 4):
             nc.scalar.dma_start(x_scales_picked[r:P:QUADRANT, :].bitcast(I32), x_scales_spread[SPREAD * r : P : QUADRANT, :].bitcast(I32))
         lay_w1(1, 1, nc.vector.tensor_copy)
-        lay_w1(0, 1, nc.scalar.copy)
+        lay_w1(0, 1, nc.vector.tensor_copy)
         w2_raw = sbuf("w2_raw", [P, PACK, N], F32, after="x_scales_spread")
         nc.sync.dma_start(w2_raw[:], w2.rearrange("(p j) c -> p j c", j=PACK))
         for g in (1, 0):

@@ -98,10 +98,10 @@ def tile_picked_carry2_none_p_kernel(tc, x_words, x_scales, w1, w2, offs, s1, d1
         half_d = [sbuf("half_d%d" % t, [P, V], F32) for t in range(PACK)]
         z_bf = [sbuf("z_bf%d" % n, [P, width, PACK], BF16) for n, (start, width) in enumerate(Z_PIECES)]
 
-        def project(t, start, width, copy, first_bank, banks_taken=1):
+        def project(t, start, width, copy, number):
             places = slice(start, start + width)
             columns = slice(P * (t % 2), P * (t % 2 + 1))
-            acc = bank("y%d_%d" % (t, start), first_bank, banks_taken * S)[:, 0:width]
+            acc = bank("y%d_%d" % (t, start), number, width)[:]
             product(acc, w1_codes[t // 2][:, columns], w1_scales[t // 2][:, columns], x_words_picked[:, places], x_scales_picked[:, places])
             copy(plane[t][:, places], acc)
 
@@ -126,13 +126,13 @@ def tile_picked_carry2_none_p_kernel(tc, x_words, x_scales, w1, w2, offs, s1, d1
 
         for (start, width), copy, number in zip(X_PIECES, (nc.scalar.copy, nc.scalar.copy, nc.vector.tensor_copy), (0, 2, 3)):
             project(2, start, width, copy, number)
-        project(3, 0, HALF, nc.vector.tensor_copy, 0)
+        project(3, 0, HALF, nc.scalar.copy, 0)
         first_round(2)
-        project(3, HALF, HALF, nc.scalar.copy, 4, banks_taken=3)
+        project(3, HALF, HALF, nc.scalar.copy, 2)
         first_round(3)
-        project(0, 0, HALF, nc.scalar.copy, 4)
-        project(0, HALF, HALF, nc.scalar.copy, 5)
-        project(1, 0, S, nc.scalar.copy, 6)
+        project(0, 0, HALF, nc.scalar.copy, 3)
+        project(0, HALF, HALF, nc.scalar.copy, 0)
+        project(1, 0, S, nc.scalar.copy, 2)
 
         w2_bf = [sbuf("w2_bf%d" % h, [P, HALF, PACK], BF16) for h in range(2)]
         for h in range(2):

@@ -118,7 +118,11 @@ def tile_picked_carry2_none_p_kernel(tc, x_words, x_scales, w1, w2, offs, s1, d1
             nc.scalar.activation(half_d[t][:], plane[t][:].indirect(d2_t[:]), COPY, scale=0.5)
 
         def put_means(t):
-            nc.vector.tensor_tensor(plane[t][:].indirect(d2_t[:]), half_s[t][:], half_d[t][:], ADD)
+            nc.gpsimd.tensor_tensor(means[:, V * t : V * (t + 1)], half_s[t][:], half_d[t][:], ADD)
+            nc.vector.tensor_copy(plane[t][:].indirect(d2_t[:]), means[:, V * t : V * (t + 1)])
+
+        def gpsimd_copy(dst, src):
+            nc.gpsimd.tensor_scalar(dst, src, 1.0, 0.0, op0=MULT, op1=ADD)
 
         def round_pair(u, n, copy):
             start, width = Z_PIECES[n]
@@ -137,8 +141,9 @@ def tile_picked_carry2_none_p_kernel(tc, x_words, x_scales, w1, w2, offs, s1, d1
         w2_bf = [sbuf("w2_bf%d" % h, [P, HALF, PACK], BF16) for h in range(2)]
         for h in range(2):
             src = w2_raw[:, :, HALF * h : HALF * (h + 1)].rearrange("p (i u) c -> p c u i", i=2)
-            nc.gpsimd.tensor_scalar(w2_bf[h][:].rearrange("p c (u i) -> p c u i", i=2), src, 1.0, 0.0, op0=MULT, op1=ADD)
+            gpsimd_copy(w2_bf[h][:].rearrange("p c (u i) -> p c u i", i=2), src)
 
+        means = sbuf("means", [P, PACK * V], F32, after="x_scales_spread")
         for u in range(2):
             first_round(u)
         for u in range(2):
@@ -146,6 +151,7 @@ def tile_picked_carry2_none_p_kernel(tc, x_words, x_scales, w1, w2, offs, s1, d1
             put_means(2 + u)
         for u in range(2):
             fetch_halves(u)
+        for u in range(2):
             nc.scalar.copy(plane[u][:, S : 2 * S], plane[2 + u][:])
             put_means(u)
         for n in range(len(Z_PIECES)):

@@ -85,7 +85,7 @@ def tile_picked_carry2_none_p_kernel(tc, x_words, x_scales, w1, w2, offs, s1, d1
             nc.scalar.dma_start(x_scales_picked[r:P:QUADRANT, :].bitcast(I32), x_scales_spread[SPREAD * r : P : QUADRANT, :].bitcast(I32))
         lay_w1(1, 1, nc.vector.tensor_copy)
         lay_w1(0, 1, nc.vector.tensor_copy)
-        w2_raw = sbuf("w2_raw", [P, PACK, N], F32, after="x_scales_spread")
+        w2_raw = sbuf("w2_raw", [P, PACK, N], F32, after="w1_raw1")
         nc.sync.dma_start(w2_raw[:], w2.rearrange("(p j) c -> p j c", j=PACK))
         for g in (1, 0):
             quantise(w1_codes[g][:], w1_scales[g][:], w1_bf[g][:].rearrange("p u m j -> p (u m j)"))
@@ -94,8 +94,6 @@ def tile_picked_carry2_none_p_kernel(tc, x_words, x_scales, w1, w2, offs, s1, d1
 
         plane = [sbuf("plane%d" % t, [P, 2 * S if t < 2 else S], F32) for t in range(PACK)]
         moved = [sbuf("moved%d" % t, [P, V], F32) for t in range(PACK)]
-        half_s = [sbuf("half_s%d" % t, [P, V], F32) for t in range(PACK)]
-        half_d = [sbuf("half_d%d" % t, [P, V], F32) for t in range(PACK)]
         z_bf = [sbuf("z_bf%d" % n, [P, width, PACK], BF16) for n, (start, width) in enumerate(Z_PIECES)]
 
         def project(t, start, width, copy, number):
@@ -105,72 +103,88 @@ def tile_picked_carry2_none_p_kernel(tc, x_words, x_scales, w1, w2, offs, s1, d1
             product(acc, w1_codes[t // 2][:, columns], w1_scales[t // 2][:, columns], x_words_picked[:, places], x_scales_picked[:, places])
             copy(plane[t][:, places], acc)
 
-        def first_round(t):
-            if t == 2:
-                nc.vector.tensor_copy(moved[t][:, 0:P], plane[t][:].indirect(s1_t[:, 0 : P // 16]))
-                nc.scalar.activation(moved[t][:, P:V], plane[t][:].indirect(s1_t[:, P // 16 : V // 16]), COPY)
+        def scalar_move(dst, src, scale=1.0):
+            nc.scalar.activation(dst, src, COPY, scale=scale)
+
+        def vector_move(dst, src, scale=1.0):
+            if scale == 1.0:
+                nc.vector.tensor_copy(dst, src)
             else:
-                nc.scalar.activation(moved[t][:], plane[t][:].indirect(s1_t[:]), COPY)
-            nc.vector.tensor_copy(plane[t][:].indirect(d1_t[:]), moved[t][:])
-
-        def fetch_halves(t):
-            nc.scalar.activation(half_s[t][:], plane[t][:].indirect(s2_t[:]), COPY, scale=0.5)
-            nc.scalar.activation(half_d[t][:], plane[t][:].indirect(d2_t[:]), COPY, scale=0.5)
-
-        def put_means(t):
-            nc.gpsimd.tensor_tensor(means[:, V * t : V * (t + 1)], half_s[t][:], half_d[t][:], ADD)
-            nc.vector.tensor_copy(plane[t][:].indirect(d2_t[:]), means[:, V * t : V * (t + 1)])
+                nc.vector.tensor_scalar(dst, src, scale, 0.0, op0=MULT, op1=ADD)
 
         def gpsimd_copy(dst, src):
             nc.gpsimd.tensor_scalar(dst, src, 1.0, 0.0, op0=MULT, op1=ADD)
+
+        def at(t, offsets):
+            return plane[t][:].indirect(offsets[:])
 
         def round_pair(u, n, copy):
             start, width = Z_PIECES[n]
             copy(z_bf[n][:, :, 2 * u : 2 * u + 2], plane[u][:].rearrange("p (i s) -> p s i", i=2)[:, start : start + width, :])
 
-        for (start, width), copy, number in zip(X_PIECES, (nc.scalar.copy, nc.scalar.copy, nc.vector.tensor_copy), (0, 2, 3)):
-            project(2, start, width, copy, number)
-        project(3, 0, HALF, nc.scalar.copy, 0)
-        first_round(2)
-        project(3, HALF, HALF, nc.scalar.copy, 2)
-        first_round(3)
-        project(0, 0, HALF, nc.scalar.copy, 3)
-        project(0, HALF, HALF, nc.scalar.copy, 0)
-        project(1, 0, S, nc.scalar.copy, 2)
+        for number, (start, width) in enumerate(X_PIECES):
+            project(2, start, width, nc.scalar.copy, number)
+        project(3, 0, HALF, nc.vector.tensor_copy, 3)
+        project(3, HALF, HALF, nc.vector.tensor_copy, 4)
+        scalar_move(moved[2][:], at(2, s1_t))
+        vector_move(moved[3][:], at(3, s1_t))
+        project(0, 0, HALF, nc.scalar.copy, 5)
+        project(0, HALF, HALF, nc.scalar.copy, 6)
+        project(1, 0, HALF, nc.vector.tensor_copy, 7)
+        scalar_move(at(2, d1_t), moved[2][:])
+        vector_move(at(3, d1_t), moved[3][:])
+        project(1, HALF, HALF, nc.scalar.copy, 0)
 
-        w2_bf = [sbuf("w2_bf%d" % h, [P, HALF, PACK], BF16) for h in range(2)]
-        for h in range(2):
-            src = w2_raw[:, :, HALF * h : HALF * (h + 1)].rearrange("p (i u) c -> p c u i", i=2)
-            gpsimd_copy(w2_bf[h][:].rearrange("p c (u i) -> p c u i", i=2), src)
+        w2_bf = sbuf("w2_bf", [P, N, PACK], BF16)
+        gpsimd_copy(w2_bf[:].rearrange("p c (u i) -> p c u i", i=2), w2_raw[:].rearrange("p (i u) c -> p c u i", i=2))
 
-        means = sbuf("means", [P, PACK * V], F32, after="x_scales_spread")
-        for u in range(2):
-            first_round(u)
-        for u in range(2):
-            fetch_halves(2 + u)
-            put_means(2 + u)
-        for u in range(2):
-            fetch_halves(u)
-        for u in range(2):
-            nc.scalar.copy(plane[u][:, S : 2 * S], plane[2 + u][:])
-            put_means(u)
-        for n in range(len(Z_PIECES)):
-            round_pair(0, n, nc.scalar.copy)
+        from_s = [sbuf("from_s%d" % t, [P, V], F32)[:] for t in (1, 2, 3)]
+        from_d = [sbuf("from_d%d" % t, [P, V], F32)[:] for t in range(PACK)]
+        behind_w2 = sbuf("behind_w2", [P, 2 * V], F32, after="w1_raw1")
+        from_s = [behind_w2[:, 0:V]] + from_s
+        means = [sbuf("means0", [P, V], F32)[:], from_s[0], from_d[2], behind_w2[:, V : 2 * V]]
 
-        w2_codes = [sbuf("w2_codes%d" % h, [P, HALF], U32, after=after) for h, after in enumerate(("plane3", "z_bf0"))]
+        def add_halves(t):
+            nc.gpsimd.tensor_tensor(means[t], from_s[t], from_d[t], ADD)
+
+        vector_move(moved[0][:], at(0, s1_t))
+        scalar_move(from_s[2], at(2, s2_t))
+        vector_move(from_s[3], at(3, s2_t), 0.5)
+        scalar_move(moved[1][:], at(1, s1_t))
+        vector_move(at(0, d1_t), moved[0][:])
+        scalar_move(from_d[3], at(3, d2_t), 0.5)
+        add_halves(3)
+        scalar_move(at(1, d1_t), moved[1][:])
+        nc.vector.tensor_tensor(from_d[2], at(2, d2_t), from_s[2], ADD)
+        vector_move(from_s[0], at(0, s2_t), 0.5)
+        scalar_move(from_d[0], at(0, d2_t), 0.5)
+        add_halves(0)
+        vector_move(at(3, d2_t), means[3])
+        scalar_move(from_s[1], at(1, s2_t), 0.5)
+        scalar_move(from_d[1], at(1, d2_t), 0.5)
+        add_halves(1)
+        gpsimd_copy(plane[1][:, S : 2 * S], plane[3][:])
+        scalar_move(at(2, d2_t), means[2], 0.5)
+        vector_move(at(0, d2_t), means[0])
+        scalar_move(at(1, d2_t), means[1])
+
+        w2_codes = [sbuf("w2_codes%d" % h, [P, HALF], U32, after=after) for h, after in enumerate(("means0", "z_bf0"))]
         w2_scales = [sbuf("w2_scales%d" % h, [P, HALF], U8) for h in range(2)]
         z_codes = [sbuf("z_codes%d" % h, [P, HALF], U32) for h in range(2)]
         z_scales = [sbuf("z_scales%d" % h, [P, HALF], U8) for h in range(2)]
 
         def quantise_w2(h):
-            quantise(w2_codes[h][:], w2_scales[h][:], w2_bf[h][:].rearrange("p c j -> p (c j)"))
+            quantise(w2_codes[h][:], w2_scales[h][:], w2_bf[:, HALF * h : HALF * (h + 1), :].rearrange("p c j -> p (c j)"))
 
         def quantise_z(n):
             start, width = Z_PIECES[n]
             places = slice(start % HALF, start % HALF + width)
             quantise(z_codes[start // HALF][:, places], z_scales[start // HALF][:, places], z_bf[n][:].rearrange("p s j -> p (s j)"))
 
+        nc.vector.tensor_copy(plane[0][:, S : 2 * S], plane[2][:])
         quantise_w2(0)
+        for n in range(len(Z_PIECES)):
+            round_pair(0, n, nc.vector.tensor_copy)
         round_pair(1, 0, nc.vector.tensor_copy)
         round_pair(1, 1, nc.vector.tensor_copy)
         round_pair(1, 2, nc.scalar.copy)

@@ -31,10 +31,14 @@ def tile_picked_carry2_none_p_kernel(tc, x_words, x_scales, w1, w2, offs, s1, d1
     with ExitStack() as ctx:
         lists = ctx.enter_context(tc.tile_pool(name="lists", bufs=1))
         keep = ctx.enter_context(tc.tile_pool(name="keep", bufs=1))
+        shared = ctx.enter_context(tc.tile_pool(name="shared", bufs=1))
         psum = ctx.enter_context(tc.psum_pool(name="psum", bufs=1))
 
         def sbuf(name, shape, dtype, after=None):
             return keep.tile(shape, dtype, name=name, tag=after or name, align_bytes=64)
+
+        def overlaid(name, shape, dtype, offset):
+            return shared.tile(shape, dtype, name=name, offset=offset, align_bytes=64)
 
         def bank(name, number, width):
             return psum.tile([P, width], F32, name=name, offset=BANK_BYTES * number)
@@ -54,7 +58,7 @@ def tile_picked_carry2_none_p_kernel(tc, x_words, x_scales, w1, w2, offs, s1, d1
         x_scale_rows = sbuf("x_scale_rows", [P, T], U8)
         nc.vector.memset(x_scale_rows[:].bitcast(I32), 0)
         x_word_rows = sbuf("x_word_rows", [P, T], U32)
-        w1_raw = [sbuf("w1_raw%d" % e, [P, 2, H], F32) for e in range(2)]
+        w1_raw = [sbuf("w1_raw0", [P, 2, H], F32), overlaid("w1_raw1", [P, 2, H], F32, 0)]
 
         w1_v = w1.rearrange("(p j) c -> p j c", j=PACK)
         nc.sync.dma_start(w1_raw[0][:], w1_v[:, 0:2, :])
@@ -69,9 +73,11 @@ def tile_picked_carry2_none_p_kernel(tc, x_words, x_scales, w1, w2, offs, s1, d1
         w1_codes = [sbuf("w1_codes%d" % g, [P, 2 * P], U32) for g in range(2)]
         w1_scales = [sbuf("w1_scales%d" % g, [P, 2 * P], U8) for g in range(2)]
 
-        def lay_w1(g, e, copy):
+        def lay_w1(g, e, copy, width=P):
             src = w1_raw[e][:].rearrange("p j (m t) -> p m j t", t=PACK)[:, :, :, 2 * g : 2 * g + 2]
-            copy(w1_bf[g][:, :, :, 2 * e : 2 * e + 2].rearrange("p u m j -> p m j u"), src)
+            dst = w1_bf[g][:, :, :, 2 * e : 2 * e + 2].rearrange("p u m j -> p m j u")
+            for start in range(0, P, width):
+                copy(dst[:, start : start + width], src[:, start : start + width])
 
         x_scales_spread = sbuf("x_scales_spread", [P, S], U8)
         x_scales_picked = sbuf("x_scales_picked", [P, S], U8)
@@ -83,18 +89,19 @@ def tile_picked_carry2_none_p_kernel(tc, x_words, x_scales, w1, w2, offs, s1, d1
         nc.vector.tensor_copy(x_scales_picked[:].bitcast(I32), x_scales_spread[:].bitcast(I32))
         for r in range(1, 4):
             nc.scalar.dma_start(x_scales_picked[r:P:QUADRANT, :].bitcast(I32), x_scales_spread[SPREAD * r : P : QUADRANT, :].bitcast(I32))
-        lay_w1(1, 1, nc.vector.tensor_copy)
-        lay_w1(0, 1, nc.vector.tensor_copy)
-        w2_raw = sbuf("w2_raw", [P, PACK, N], F32, after="w1_raw1")
+        lay_w1(1, 1, nc.vector.tensor_copy, 32)
+        lay_w1(0, 1, nc.vector.tensor_copy, 16)
+        w2_raw = overlaid("w2_raw", [P, PACK, N], F32, 0)
         nc.sync.dma_start(w2_raw[:], w2.rearrange("(p j) c -> p j c", j=PACK))
         for g in (1, 0):
-            quantise(w1_codes[g][:], w1_scales[g][:], w1_bf[g][:].rearrange("p u m j -> p (u m j)"))
+            for u in range(2):
+                columns = slice(P * u, P * (u + 1))
+                quantise(w1_codes[g][:, columns], w1_scales[g][:, columns], w1_bf[g][:, u].rearrange("p m j -> p (m j)"))
         for start, width in X_PIECES:
             nc.vector.tensor_copy(x_words_picked[:, start : start + width], x_word_rows[:].indirect(offs_t[:, start // 16 : (start + width) // 16]))
 
         plane = [sbuf("plane%d" % t, [P, 2 * S if t < 2 else S], F32) for t in range(PACK)]
         moved = [sbuf("moved%d" % t, [P, V], F32) for t in range(PACK)]
-        z_bf = [sbuf("z_bf%d" % n, [P, width, PACK], BF16) for n, (start, width) in enumerate(Z_PIECES)]
 
         def project(t, start, width, copy, number):
             places = slice(start, start + width)
@@ -122,14 +129,14 @@ def tile_picked_carry2_none_p_kernel(tc, x_words, x_scales, w1, w2, offs, s1, d1
             start, width = Z_PIECES[n]
             copy(z_bf[n][:, :, 2 * u : 2 * u + 2], plane[u][:].rearrange("p (i s) -> p s i", i=2)[:, start : start + width, :])
 
-        for number, (start, width) in enumerate(X_PIECES):
-            project(2, start, width, nc.scalar.copy, number)
-        project(3, 0, HALF, nc.vector.tensor_copy, 3)
+        for number, ((start, width), copy) in enumerate(zip(X_PIECES, (nc.scalar.copy, nc.vector.tensor_copy, nc.vector.tensor_copy))):
+            project(2, start, width, copy, number)
+        project(3, 0, HALF, nc.scalar.copy, 3)
         project(3, HALF, HALF, nc.vector.tensor_copy, 4)
         scalar_move(moved[2][:], at(2, s1_t))
-        vector_move(moved[3][:], at(3, s1_t))
-        project(0, 0, HALF, nc.scalar.copy, 5)
+        project(0, 0, HALF, nc.vector.tensor_copy, 5)
         project(0, HALF, HALF, nc.scalar.copy, 6)
+        vector_move(moved[3][:], at(3, s1_t))
         project(1, 0, HALF, nc.vector.tensor_copy, 7)
         scalar_move(at(2, d1_t), moved[2][:])
         vector_move(at(3, d1_t), moved[3][:])
@@ -138,13 +145,11 @@ def tile_picked_carry2_none_p_kernel(tc, x_words, x_scales, w1, w2, offs, s1, d1
         w2_bf = sbuf("w2_bf", [P, N, PACK], BF16)
         gpsimd_copy(w2_bf[:].rearrange("p c (u i) -> p c u i", i=2), w2_raw[:].rearrange("p (i u) c -> p c u i", i=2))
 
-        from_s = [sbuf("from_s%d" % t, [P, V], F32)[:] for t in (1, 2, 3)]
-        from_d = [sbuf("from_d%d" % t, [P, V], F32)[:] for t in range(PACK)]
-        behind_w2 = sbuf("behind_w2", [P, 2 * V], F32, after="w1_raw1")
-        from_s = [behind_w2[:, 0:V]] + from_s
-        means = [sbuf("means0", [P, V], F32)[:], from_s[0], from_d[2], behind_w2[:, V : 2 * V]]
+        from_s = [overlaid("from_s0", [P, V], F32, 6144)[:]] + [sbuf("from_s%d" % t, [P, V], F32)[:] for t in (1, 2, 3)]
+        from_d = [overlaid("from_d2", [P, V], F32, 5120)[:] if t == 2 else sbuf("from_d%d" % t, [P, V], F32)[:] for t in range(PACK)]
+        means = [overlaid("means%d" % t, [P, V], F32, offset)[:] for t, offset in enumerate((0, 5120, 3072, 2048))]
 
-        def add_halves(t):
+        def add_up(t):
             nc.gpsimd.tensor_tensor(means[t], from_s[t], from_d[t], ADD)
 
         vector_move(moved[0][:], at(0, s1_t))
@@ -153,54 +158,57 @@ def tile_picked_carry2_none_p_kernel(tc, x_words, x_scales, w1, w2, offs, s1, d1
         scalar_move(moved[1][:], at(1, s1_t))
         vector_move(at(0, d1_t), moved[0][:])
         scalar_move(from_d[3], at(3, d2_t), 0.5)
-        add_halves(3)
+        add_up(3)
         scalar_move(at(1, d1_t), moved[1][:])
-        nc.vector.tensor_tensor(from_d[2], at(2, d2_t), from_s[2], ADD)
+        vector_move(from_d[2], at(2, d2_t))
+        add_up(2)
         vector_move(from_s[0], at(0, s2_t), 0.5)
         scalar_move(from_d[0], at(0, d2_t), 0.5)
-        add_halves(0)
+        add_up(0)
         vector_move(at(3, d2_t), means[3])
-        scalar_move(from_s[1], at(1, s2_t), 0.5)
-        scalar_move(from_d[1], at(1, d2_t), 0.5)
-        add_halves(1)
+        scalar_move(from_s[1], at(1, s2_t))
+        scalar_move(from_d[1], at(1, d2_t))
+        add_up(1)
         gpsimd_copy(plane[1][:, S : 2 * S], plane[3][:])
         scalar_move(at(2, d2_t), means[2], 0.5)
         vector_move(at(0, d2_t), means[0])
-        scalar_move(at(1, d2_t), means[1])
+        scalar_move(at(1, d2_t), means[1], 0.5)
 
-        w2_codes = [sbuf("w2_codes%d" % h, [P, HALF], U32, after=after) for h, after in enumerate(("means0", "z_bf0"))]
-        w2_scales = [sbuf("w2_scales%d" % h, [P, HALF], U8) for h in range(2)]
+        z_bf = [sbuf("z_bf%d" % n, [P, P, PACK], BF16) for n in range(2)] + [overlaid("z_bf2", [P, HALF, PACK], BF16, 4096)]
+        w2_codes = overlaid("w2_codes", [P, N], U32, 0)
+        w2_scales = sbuf("w2_scales", [P, N], U8)
         z_codes = [sbuf("z_codes%d" % h, [P, HALF], U32) for h in range(2)]
         z_scales = [sbuf("z_scales%d" % h, [P, HALF], U8) for h in range(2)]
 
         def quantise_w2(h):
-            quantise(w2_codes[h][:], w2_scales[h][:], w2_bf[:, HALF * h : HALF * (h + 1), :].rearrange("p c j -> p (c j)"))
+            columns = slice(HALF * h, HALF * (h + 1))
+            quantise(w2_codes[:, columns], w2_scales[:, columns], w2_bf[:, columns, :].rearrange("p c j -> p (c j)"))
 
         def quantise_z(n):
             start, width = Z_PIECES[n]
             places = slice(start % HALF, start % HALF + width)
             quantise(z_codes[start // HALF][:, places], z_scales[start // HALF][:, places], z_bf[n][:].rearrange("p s j -> p (s j)"))
 
-        nc.vector.tensor_copy(plane[0][:, S : 2 * S], plane[2][:])
         quantise_w2(0)
-        for n in range(len(Z_PIECES)):
-            round_pair(0, n, nc.vector.tensor_copy)
-        round_pair(1, 0, nc.vector.tensor_copy)
-        round_pair(1, 1, nc.vector.tensor_copy)
+        nc.vector.tensor_copy(plane[0][:, S : 2 * S], plane[2][:])
+        quantise_w2(1)
+        for u in range(2):
+            for n in range(2):
+                round_pair(u, n, nc.vector.tensor_copy)
         round_pair(1, 2, nc.scalar.copy)
         quantise_z(0)
         quantise_z(1)
-        quantise_w2(1)
+        round_pair(0, 2, nc.vector.tensor_copy)
         quantise_z(2)
 
         out_v = out.rearrange("(b p) s -> p b s", p=P)
         banks_in_turn = [n % BANKS for n in range(11, 0, -1)]
 
         def result(b, start, width, copy, staged):
-            columns = slice(P * (b % 2), P * (b % 2 + 1))
+            columns = slice(P * b, P * (b + 1))
             places = slice(start % HALF, start % HALF + width)
             acc = bank("out%d_%d" % (b, start), banks_in_turn.pop(), width)
-            product(acc[:], w2_codes[b // 2][:, columns], w2_scales[b // 2][:, columns], z_codes[start // HALF][:, places], z_scales[start // HALF][:, places])
+            product(acc[:], w2_codes[:, columns], w2_scales[:, columns], z_codes[start // HALF][:, places], z_scales[start // HALF][:, places])
             copy(staged, acc[:])
 
         def stored(b, start, width, copy):

@@ -89,7 +89,7 @@ def tile_picked_carry2_none_p_kernel(tc, x_words, x_scales, w1, w2, offs, s1, d1
         nc.vector.tensor_copy(x_scales_picked[:].bitcast(I32), x_scales_spread[:].bitcast(I32))
         for r in range(1, 4):
             nc.scalar.dma_start(x_scales_picked[r:P:QUADRANT, :].bitcast(I32), x_scales_spread[SPREAD * r : P : QUADRANT, :].bitcast(I32))
-        lay_w1(1, 1, nc.vector.tensor_copy, 32)
+        lay_w1(1, 1, nc.vector.tensor_copy, 64)
         lay_w1(0, 1, nc.vector.tensor_copy, 16)
         w2_raw = overlaid("w2_raw", [P, PACK, N], F32, 0)
         nc.sync.dma_start(w2_raw[:], w2.rearrange("(p j) c -> p j c", j=PACK))
@@ -175,7 +175,7 @@ def tile_picked_carry2_none_p_kernel(tc, x_words, x_scales, w1, w2, offs, s1, d1
         scalar_move(at(1, d2_t), means[1], 0.5)
 
         z_bf = [sbuf("z_bf%d" % n, [P, P, PACK], BF16) for n in range(2)] + [overlaid("z_bf2", [P, HALF, PACK], BF16, 4096)]
-        w2_codes = overlaid("w2_codes", [P, N], U32, 0)
+        w2_codes = sbuf("w2_codes", [P, N], U32, after="from_s1")
         w2_scales = sbuf("w2_scales", [P, N], U8)
         z_codes = [sbuf("z_codes%d" % h, [P, HALF], U32) for h in range(2)]
         z_scales = [sbuf("z_scales%d" % h, [P, HALF], U8) for h in range(2)]

@@ -22,7 +22,7 @@ HALF = 256
 QUADRANT = 32
 SPREAD = 8
 BANKS, BANK_BYTES = 8, 2048
-X_PIECES = ((0, 256), (256, 128), (384, 128))
+X_PIECES = ((0, 128), (128, 128), (256, 128), (384, 128))
 Z_PIECES = ((0, 128), (128, 128), (256, 256))
 
 
@@ -129,18 +129,26 @@ def tile_picked_carry2_none_p_kernel(tc, x_words, x_scales, w1, w2, offs, s1, d1
             start, width = Z_PIECES[n]
             copy(z_bf[n][:, :, 2 * u : 2 * u + 2], plane[u][:].rearrange("p (i s) -> p s i", i=2)[:, start : start + width, :])
 
-        for number, ((start, width), copy) in enumerate(zip(X_PIECES, (nc.scalar.copy, nc.vector.tensor_copy, nc.vector.tensor_copy))):
-            project(2, start, width, copy, number)
-        project(3, 0, HALF, nc.scalar.copy, 3)
-        project(3, HALF, HALF, nc.vector.tensor_copy, 4)
+        first = {t: bank("y%d_first" % t, t - 2, HALF) for t in (2, 3)}
+        engines = ((2, nc.scalar.copy), (3, nc.vector.tensor_copy))
+        for start in (0, P):
+            for t, copy in engines:
+                columns = slice(P * (t % 2), P * (t % 2 + 1))
+                places = slice(start, start + P)
+                product(first[t][:, places], w1_codes[1][:, columns], w1_scales[1][:, columns], x_words_picked[:, places], x_scales_picked[:, places])
+        for t, copy in engines:
+            copy(plane[t][:, 0:HALF], first[t][:])
+        for n, start in enumerate((HALF, HALF + P)):
+            for t, copy in engines:
+                project(t, start, P, copy, 2 * n + t)
         scalar_move(moved[2][:], at(2, s1_t))
-        project(0, 0, HALF, nc.vector.tensor_copy, 5)
-        project(0, HALF, HALF, nc.scalar.copy, 6)
+        project(0, 0, HALF, nc.vector.tensor_copy, 6)
+        project(0, HALF, HALF, nc.scalar.copy, 7)
         vector_move(moved[3][:], at(3, s1_t))
-        project(1, 0, HALF, nc.vector.tensor_copy, 7)
+        project(1, 0, HALF, nc.vector.tensor_copy, 0)
         scalar_move(at(2, d1_t), moved[2][:])
         vector_move(at(3, d1_t), moved[3][:])
-        project(1, HALF, HALF, nc.scalar.copy, 0)
+        project(1, HALF, HALF, nc.scalar.copy, 1)
 
         w2_bf = sbuf("w2_bf", [P, N, PACK], BF16)
         gpsimd_copy(w2_bf[:].rearrange("p c (u i) -> p c u i", i=2), w2_raw[:].rearrange("p (i u) c -> p c u i", i=2))

@@ -89,14 +89,14 @@ def tile_picked_carry2_none_p_kernel(tc, x_words, x_scales, w1, w2, offs, s1, d1
         nc.vector.tensor_copy(x_scales_picked[:].bitcast(I32), x_scales_spread[:].bitcast(I32))
         for r in range(1, 4):
             nc.scalar.dma_start(x_scales_picked[r:P:QUADRANT, :].bitcast(I32), x_scales_spread[SPREAD * r : P : QUADRANT, :].bitcast(I32))
-        lay_w1(1, 1, nc.vector.tensor_copy, 64)
+        lay_w1(1, 1, nc.vector.tensor_copy)
         lay_w1(0, 1, nc.vector.tensor_copy, 16)
         w2_raw = overlaid("w2_raw", [P, PACK, N], F32, 0)
         nc.sync.dma_start(w2_raw[:], w2.rearrange("(p j) c -> p j c", j=PACK))
-        for g in (1, 0):
-            for u in range(2):
-                columns = slice(P * u, P * (u + 1))
-                quantise(w1_codes[g][:, columns], w1_scales[g][:, columns], w1_bf[g][:, u].rearrange("p m j -> p (m j)"))
+        for u in range(2):
+            columns = slice(P * u, P * (u + 1))
+            quantise(w1_codes[1][:, columns], w1_scales[1][:, columns], w1_bf[1][:, u].rearrange("p m j -> p (m j)"))
+        quantise(w1_codes[0][:], w1_scales[0][:], w1_bf[0][:].rearrange("p u m j -> p (u m j)"))
         for start, width in X_PIECES:
             nc.vector.tensor_copy(x_words_picked[:, start : start + width], x_word_rows[:].indirect(offs_t[:, start // 16 : (start + width) // 16]))
 
@@ -154,8 +154,8 @@ def tile_picked_carry2_none_p_kernel(tc, x_words, x_scales, w1, w2, offs, s1, d1
         gpsimd_copy(w2_bf[:].rearrange("p c (u i) -> p c u i", i=2), w2_raw[:].rearrange("p (i u) c -> p c u i", i=2))
 
         from_s = [overlaid("from_s0", [P, V], F32, 6144)[:]] + [sbuf("from_s%d" % t, [P, V], F32)[:] for t in (1, 2, 3)]
-        from_d = [overlaid("from_d2", [P, V], F32, 5120)[:] if t == 2 else sbuf("from_d%d" % t, [P, V], F32)[:] for t in range(PACK)]
-        means = [overlaid("means%d" % t, [P, V], F32, offset)[:] for t, offset in enumerate((0, 5120, 3072, 2048))]
+        from_d = [overlaid("from_d%d" % t, [P, V], F32, 9216 - 2048 * t)[:] if t % 2 == 0 else sbuf("from_d%d" % t, [P, V], F32)[:] for t in range(PACK)]
+        means = [overlaid("means%d" % t, [P, V], F32, offset)[:] for t, offset in enumerate((0, 9216, 3072, 2048))]
 
         def add_up(t):
             nc.gpsimd.tensor_tensor(means[t], from_s[t], from_d[t], ADD)
@@ -176,13 +176,13 @@ def tile_picked_carry2_none_p_kernel(tc, x_words, x_scales, w1, w2, offs, s1, d1
         vector_move(at(3, d2_t), means[3])
         scalar_move(from_s[1], at(1, s2_t))
         scalar_move(from_d[1], at(1, d2_t))
-        add_up(1)
+        nc.vector.tensor_tensor(means[1], from_s[1], from_d[1], ADD)
         gpsimd_copy(plane[1][:, S : 2 * S], plane[3][:])
         scalar_move(at(2, d2_t), means[2], 0.5)
         vector_move(at(0, d2_t), means[0])
         scalar_move(at(1, d2_t), means[1], 0.5)
 
-        z_bf = [sbuf("z_bf%d" % n, [P, P, PACK], BF16) for n in range(2)] + [overlaid("z_bf2", [P, HALF, PACK], BF16, 4096)]
+        z_bf = [sbuf("z_bf%d" % n, [P, P, PACK], BF16) for n in range(2)] + [overlaid("z_bf2", [P, HALF, PACK], BF16, 8192)]
         w2_codes = sbuf("w2_codes", [P, N], U32, after="from_s1")
         w2_scales = sbuf("w2_scales", [P, N], U8)
         z_codes = [sbuf("z_codes%d" % h, [P, HALF], U32) for h in range(2)]

@@ -89,8 +89,8 @@ def tile_picked_carry2_none_p_kernel(tc, x_words, x_scales, w1, w2, offs, s1, d1
         nc.vector.tensor_copy(x_scales_picked[:].bitcast(I32), x_scales_spread[:].bitcast(I32))
         for r in range(1, 4):
             nc.scalar.dma_start(x_scales_picked[r:P:QUADRANT, :].bitcast(I32), x_scales_spread[SPREAD * r : P : QUADRANT, :].bitcast(I32))
-        lay_w1(1, 1, nc.vector.tensor_copy)
-        lay_w1(0, 1, nc.vector.tensor_copy, 16)
+        lay_w1(1, 1, nc.vector.tensor_copy, 64)
+        lay_w1(0, 1, nc.vector.tensor_copy, 32)
         w2_raw = overlaid("w2_raw", [P, PACK, N], F32, 0)
         nc.sync.dma_start(w2_raw[:], w2.rearrange("(p j) c -> p j c", j=PACK))
         for u in range(2):
@@ -161,7 +161,8 @@ def tile_picked_carry2_none_p_kernel(tc, x_words, x_scales, w1, w2, offs, s1, d1
             nc.gpsimd.tensor_tensor(means[t], from_s[t], from_d[t], ADD)
 
         vector_move(moved[0][:], at(0, s1_t))
-        scalar_move(from_s[2], at(2, s2_t))
+        vector_move(from_s[2][:, 0:P], plane[2][:].indirect(s2_t[:, 0 : P // 16]))
+        scalar_move(from_s[2][:, P:V], plane[2][:].indirect(s2_t[:, P // 16 : V // 16]))
         vector_move(from_s[3], at(3, s2_t), 0.5)
         scalar_move(moved[1][:], at(1, s1_t))
         vector_move(at(0, d1_t), moved[0][:])
@@ -206,11 +207,15 @@ def tile_picked_carry2_none_p_kernel(tc, x_words, x_scales, w1, w2, offs, s1, d1
         round_pair(1, 2, nc.scalar.copy)
         quantise_z(0)
         quantise_z(1)
-        round_pair(0, 2, nc.vector.tensor_copy)
-        quantise_z(2)
+        upper = plane[0][:].rearrange("p (i s) -> p s i", i=2)
+        for start in (0, P):
+            nc.vector.tensor_copy(z_bf[2][:, start : start + P, 0:2], upper[:, HALF + start : HALF + start + P, :])
+        for start in (0, P):
+            places = slice(start, start + P)
+            quantise(z_codes[1][:, places], z_scales[1][:, places], z_bf[2][:, places, :].rearrange("p s j -> p (s j)"))
 
         out_v = out.rearrange("(b p) s -> p b s", p=P)
-        banks_in_turn = [n % BANKS for n in range(11, 0, -1)]
+        banks_in_turn = [n % BANKS for n in range(12, 0, -1)]
 
         def result(b, start, width, copy, staged):
             columns = slice(P * b, P * (b + 1))
@@ -232,7 +237,10 @@ def tile_picked_carry2_none_p_kernel(tc, x_words, x_scales, w1, w2, offs, s1, d1
         nc.sync.dma_start(out_v[:, 1, 0:HALF], staged_1[:])
         stored(2, 0, HALF, nc.scalar.copy)
         stored(3, 0, HALF, nc.vector.tensor_copy)
-        stored(0, HALF, HALF, nc.scalar.copy)
+        staged_0 = sbuf("staged_0", [P, HALF], F32)
+        result(0, HALF, P, nc.scalar.copy, staged_0[:, 0:P])
+        result(0, HALF + P, P, nc.scalar.copy, staged_0[:, P:HALF])
+        nc.sync.dma_start(out_v[:, 0, HALF:S], staged_0[:])
         stored(1, HALF, HALF, nc.vector.tensor_copy)
         stored(2, HALF, HALF, nc.scalar.copy)
         staged_last = sbuf("staged_last", [P, HALF], F32)

@@ -35,10 +35,10 @@ def tile_picked_carry2_none_p_kernel(tc, x_words, x_scales, w1, w2, offs, s1, d1
         psum = ctx.enter_context(tc.psum_pool(name="psum", bufs=1))
 
         def sbuf(name, shape, dtype, after=None):
-            return keep.tile(shape, dtype, name=name, tag=after or name, align_bytes=64)
+            return keep.tile(shape, dtype, name=name, tag=after or name, align_bytes=256)
 
         def overlaid(name, shape, dtype, offset):
-            return shared.tile(shape, dtype, name=name, offset=offset, align_bytes=64)
+            return shared.tile(shape, dtype, name=name, offset=offset, align_bytes=256)
 
         def bank(name, number, width):
             return psum.tile([P, width], F32, name=name, offset=BANK_BYTES * number)
@@ -142,8 +142,12 @@ def tile_picked_carry2_none_p_kernel(tc, x_words, x_scales, w1, w2, offs, s1, d1
             for t, copy in engines:
                 project(t, start, P, copy, 2 * n + t)
         scalar_move(moved[2][:], at(2, s1_t))
-        project(0, 0, HALF, nc.vector.tensor_copy, 6)
-        project(0, HALF, HALF, nc.scalar.copy, 7)
+        project(0, 0, P, nc.vector.tensor_copy, 6)
+        rest = bank("y0_rest", 7, S - P)
+        for start, width in ((P, P), (HALF, HALF)):
+            places = slice(start, start + width)
+            product(rest[:, start - P : start - P + width], w1_codes[0][:, 0:P], w1_scales[0][:, 0:P], x_words_picked[:, places], x_scales_picked[:, places])
+        nc.scalar.copy(plane[0][:, P:S], rest[:])
         vector_move(moved[3][:], at(3, s1_t))
         project(1, 0, HALF, nc.vector.tensor_copy, 0)
         scalar_move(at(2, d1_t), moved[2][:])
@@ -215,7 +219,7 @@ def tile_picked_carry2_none_p_kernel(tc, x_words, x_scales, w1, w2, offs, s1, d1
             quantise(z_codes[1][:, places], z_scales[1][:, places], z_bf[2][:, places, :].rearrange("p s j -> p (s j)"))
 
         out_v = out.rearrange("(b p) s -> p b s", p=P)
-        banks_in_turn = [n % BANKS for n in range(12, 0, -1)]
+        banks_in_turn = [n % BANKS for n in range(11, 0, -1)]
 
         def result(b, start, width, copy, staged):
             columns = slice(P * b, P * (b + 1))
@@ -230,11 +234,8 @@ def tile_picked_carry2_none_p_kernel(tc, x_words, x_scales, w1, w2, offs, s1, d1
             nc.sync.dma_start(out_v[:, b, start : start + width], staged[:])
 
         stored(0, 0, P, nc.scalar.copy)
-        staged_1 = sbuf("staged_1", [P, HALF], F32)
-        result(1, 0, P, nc.scalar.copy, staged_1[:, 0:P])
         stored(0, P, P, nc.scalar.copy)
-        result(1, P, P, nc.scalar.copy, staged_1[:, P:HALF])
-        nc.sync.dma_start(out_v[:, 1, 0:HALF], staged_1[:])
+        stored(1, 0, HALF, nc.scalar.copy)
         stored(2, 0, HALF, nc.scalar.copy)
         stored(3, 0, HALF, nc.vector.tensor_copy)
         staged_0 = sbuf("staged_0", [P, HALF], F32)

from contextlib import ExitStack

import concourse.mybir as mybir

K, T, S, V, H, N = 512, 2048, 512, 256, 512, 512
FLOPS = 2 * K * H * S + 2 * H * N * S

F32 = mybir.dt.float32
BF16 = mybir.dt.bfloat16
I32 = mybir.dt.int32
U32 = mybir.dt.uint32
U16 = mybir.dt.uint16
U8 = mybir.dt.uint8
FP8X4 = mybir.dt.float8_e4m3fn_x4
COPY = mybir.ActivationFunctionType.Copy
MULT = mybir.AluOpType.mult
ADD = mybir.AluOpType.add

P = 128
PACK = 4
HALF = 256
QUADRANT = 32
SPREAD = 8
BANKS, BANK_BYTES = 8, 2048
X_PIECES = ((0, 128), (128, 128), (256, 128), (384, 128))
Z_PIECES = ((0, 128), (128, 128), (256, 256))


def tile_picked_carry2_none_p_kernel(tc, x_words, x_scales, w1, w2, offs, s1, d1, s2, d2, out):
    nc = tc.nc
    with ExitStack() as ctx:
        lists = ctx.enter_context(tc.tile_pool(name="lists", bufs=1))
        keep = ctx.enter_context(tc.tile_pool(name="keep", bufs=1))
        shared = ctx.enter_context(tc.tile_pool(name="shared", bufs=1))
        psum = ctx.enter_context(tc.psum_pool(name="psum", bufs=1))

        def sbuf(name, shape, dtype, after=None):
            return keep.tile(shape, dtype, name=name, tag=after or name, align_bytes=256)

        def overlaid(name, shape, dtype, offset):
            return shared.tile(shape, dtype, name=name, offset=offset, align_bytes=256)

        def bank(name, number, width):
            return psum.tile([P, width], F32, name=name, offset=BANK_BYTES * number)

        def quantise(codes, scales, values):
            nc.vector.quantize_mx(out=codes.bitcast(FP8X4), scales=scales, in_=values)

        def product(acc, codes_l, scales_l, codes_r, scales_r):
            nc.tensor.matmul_mx(out=acc, lhsT=codes_l.bitcast(FP8X4), lhsT_scale=scales_l, rhs=codes_r.bitcast(FP8X4), rhs_scale=scales_r, start=True, stop=True)

        offs_t = lists.tile([P, S // 16], U16, name="offs_t")
        s1_t = lists.tile([P, V // 16], U16, name="s1_t")
        d1_t = lists.tile([P, V // 16], U16, name="d1_t")
        s2_t = lists.tile([P, V // 16], U16, name="s2_t")
        d2_t = lists.tile([P, V // 16], U16, name="d2_t")

        x_scale_rows = sbuf("x_scale_rows", [P, T], U8)
        nc.vector.memset(x_scale_rows[:].bitcast(I32), 0)
        x_word_rows = sbuf("x_word_rows", [P, T], U32)
        w1_raw = [sbuf("w1_raw0", [P, 2, H], F32), overlaid("w1_raw1", [P, 2, H], F32, 0)]

        w1_v = w1.rearrange("(p j) c -> p j c", j=PACK)
        nc.sync.dma_start(w1_raw[0][:], w1_v[:, 0:2, :])
        nc.sync.dma_start(offs_t[:], offs)
        nc.sync.dma_start(x_scale_rows[0:P:SPREAD, :].bitcast(I32), x_scales[0].bitcast(I32))
        nc.sync.dma_start(w1_raw[1][:], w1_v[:, 2:4, :])
        nc.sync.dma_start(x_word_rows[:].bitcast(I32), x_words[0].rearrange("p n t -> p (n t)").bitcast(I32))
        for tile, src in ((s1_t, s1), (d1_t, d1), (s2_t, s2), (d2_t, d2)):
            nc.sync.dma_start(tile[:], src)

        w1_bf = [sbuf("w1_bf%d" % g, [P, 2, P, PACK], BF16) for g in range(2)]
        w1_codes = [sbuf("w1_codes%d" % g, [P, 2 * P], U32) for g in range(2)]
        w1_scales = [sbuf("w1_scales%d" % g, [P, 2 * P], U8) for g in range(2)]

        def lay_w1(g, e, copy, width=P):
            src = w1_raw[e][:].rearrange("p j (m t) -> p m j t", t=PACK)[:, :, :, 2 * g : 2 * g + 2]
            dst = w1_bf[g][:, :, :, 2 * e : 2 * e + 2].rearrange("p u m j -> p m j u")
            for start in range(0, P, width):
                copy(dst[:, start : start + width], src[:, start : start + width])

        x_scales_spread = sbuf("x_scales_spread", [P, S], U8)
        x_scales_picked = sbuf("x_scales_picked", [P, S], U8)
        x_words_picked = sbuf("x_words_picked", [P, S], U32)

        lay_w1(1, 0, nc.scalar.copy)
        lay_w1(0, 0, nc.scalar.copy)
        nc.vector.tensor_copy(x_scales_spread[:], x_scale_rows[:].indirect(offs_t[:]))
        nc.vector.tensor_copy(x_scales_picked[:].bitcast(I32), x_scales_spread[:].bitcast(I32))
        for r in range(1, 4):
            nc.scalar.dma_start(x_scales_picked[r:P:QUADRANT, :].bitcast(I32), x_scales_spread[SPREAD * r : P : QUADRANT, :].bitcast(I32))
        lay_w1(1, 1, nc.vector.tensor_copy, 64)
        lay_w1(0, 1, nc.vector.tensor_copy, 32)
        w2_raw = overlaid("w2_raw", [P, PACK, N], F32, 0)
        nc.sync.dma_start(w2_raw[:], w2.rearrange("(p j) c -> p j c", j=PACK))
        for u in range(2):
            columns = slice(P * u, P * (u + 1))
            quantise(w1_codes[1][:, columns], w1_scales[1][:, columns], w1_bf[1][:, u].rearrange("p m j -> p (m j)"))
        quantise(w1_codes[0][:], w1_scales[0][:], w1_bf[0][:].rearrange("p u m j -> p (u m j)"))
        for start, width in X_PIECES:
            nc.vector.tensor_copy(x_words_picked[:, start : start + width], x_word_rows[:].indirect(offs_t[:, start // 16 : (start + width) // 16]))

        plane = [sbuf("plane%d" % t, [P, 2 * S if t < 2 else S], F32) for t in range(PACK)]
        moved = [sbuf("moved%d" % t, [P, V], F32) for t in range(PACK)]

        def project(t, start, width, copy, number):
            places = slice(start, start + width)
            columns = slice(P * (t % 2), P * (t % 2 + 1))
            acc = bank("y%d_%d" % (t, start), number, width)[:]
            product(acc, w1_codes[t // 2][:, columns], w1_scales[t // 2][:, columns], x_words_picked[:, places], x_scales_picked[:, places])
            copy(plane[t][:, places], acc)

        def scalar_move(dst, src, scale=1.0):
            nc.scalar.activation(dst, src, COPY, scale=scale)

        def vector_move(dst, src, scale=1.0):
            if scale == 1.0:
                nc.vector.tensor_copy(dst, src)
            else:
                nc.vector.tensor_scalar(dst, src, scale, 0.0, op0=MULT, op1=ADD)

        def gpsimd_copy(dst, src):
            nc.gpsimd.tensor_scalar(dst, src, 1.0, 0.0, op0=MULT, op1=ADD)

        def at(t, offsets):
            return plane[t][:].indirect(offsets[:])

        def round_pair(u, n, copy):
            start, width = Z_PIECES[n]
            copy(z_bf[n][:, :, 2 * u : 2 * u + 2], plane[u][:].rearrange("p (i s) -> p s i", i=2)[:, start : start + width, :])

        first = {t: bank("y%d_first" % t, t - 2, HALF) for t in (2, 3)}
        engines = ((2, nc.scalar.copy), (3, nc.vector.tensor_copy))
        for start in (0, P):
            for t, copy in engines:
                columns = slice(P * (t % 2), P * (t % 2 + 1))
                places = slice(start, start + P)
                product(first[t][:, places], w1_codes[1][:, columns], w1_scales[1][:, columns], x_words_picked[:, places], x_scales_picked[:, places])
        for t, copy in engines:
            copy(plane[t][:, 0:HALF], first[t][:])
        for n, start in enumerate((HALF, HALF + P)):
            for t, copy in engines:
                project(t, start, P, copy, 2 * n + t)
        scalar_move(moved[2][:], at(2, s1_t))
        project(0, 0, P, nc.vector.tensor_copy, 6)
        rest = bank("y0_rest", 7, S - P)
        for start, width in ((P, P), (HALF, HALF)):
            places = slice(start, start + width)
            product(rest[:, start - P : start - P + width], w1_codes[0][:, 0:P], w1_scales[0][:, 0:P], x_words_picked[:, places], x_scales_picked[:, places])
        nc.scalar.copy(plane[0][:, P:S], rest[:])
        vector_move(moved[3][:], at(3, s1_t))
        project(1, 0, HALF, nc.vector.tensor_copy, 0)
        scalar_move(at(2, d1_t), moved[2][:])
        vector_move(at(3, d1_t), moved[3][:])
        project(1, HALF, HALF, nc.scalar.copy, 1)

        w2_bf = sbuf("w2_bf", [P, N, PACK], BF16)
        gpsimd_copy(w2_bf[:].rearrange("p c (u i) -> p c u i", i=2), w2_raw[:].rearrange("p (i u) c -> p c u i", i=2))

        from_s = [overlaid("from_s0", [P, V], F32, 6144)[:]] + [sbuf("from_s%d" % t, [P, V], F32)[:] for t in (1, 2, 3)]
        from_d = [overlaid("from_d%d" % t, [P, V], F32, 9216 - 2048 * t)[:] if t % 2 == 0 else sbuf("from_d%d" % t, [P, V], F32)[:] for t in range(PACK)]
        means = [overlaid("means%d" % t, [P, V], F32, offset)[:] for t, offset in enumerate((0, 9216, 3072, 2048))]

        def add_up(t):
            nc.gpsimd.tensor_tensor(means[t], from_s[t], from_d[t], ADD)

        vector_move(moved[0][:], at(0, s1_t))
        vector_move(from_s[2][:, 0:P], plane[2][:].indirect(s2_t[:, 0 : P // 16]))
        scalar_move(from_s[2][:, P:V], plane[2][:].indirect(s2_t[:, P // 16 : V // 16]))
        vector_move(from_s[3], at(3, s2_t), 0.5)
        scalar_move(moved[1][:], at(1, s1_t))
        vector_move(at(0, d1_t), moved[0][:])
        scalar_move(from_d[3], at(3, d2_t), 0.5)
        add_up(3)
        scalar_move(at(1, d1_t), moved[1][:])
        vector_move(from_d[2], at(2, d2_t))
        add_up(2)
        vector_move(from_s[0], at(0, s2_t), 0.5)
        scalar_move(from_d[0], at(0, d2_t), 0.5)
        add_up(0)
        vector_move(at(3, d2_t), means[3])
        scalar_move(from_s[1], at(1, s2_t))
        scalar_move(from_d[1], at(1, d2_t))
        nc.vector.tensor_tensor(means[1], from_s[1], from_d[1], ADD)
        gpsimd_copy(plane[1][:, S : 2 * S], plane[3][:])
        scalar_move(at(2, d2_t), means[2], 0.5)
        vector_move(at(0, d2_t), means[0])
        scalar_move(at(1, d2_t), means[1], 0.5)

        z_bf = [sbuf("z_bf%d" % n, [P, P, PACK], BF16) for n in range(2)] + [overlaid("z_bf2", [P, HALF, PACK], BF16, 8192)]
        w2_codes = sbuf("w2_codes", [P, N], U32, after="from_s1")
        w2_scales = sbuf("w2_scales", [P, N], U8)
        z_codes = [sbuf("z_codes%d" % h, [P, HALF], U32) for h in range(2)]
        z_scales = [sbuf("z_scales%d" % h, [P, HALF], U8) for h in range(2)]

        def quantise_w2(h):
            columns = slice(HALF * h, HALF * (h + 1))
            quantise(w2_codes[:, columns], w2_scales[:, columns], w2_bf[:, columns, :].rearrange("p c j -> p (c j)"))

        def quantise_z(n):
            start, width = Z_PIECES[n]
            places = slice(start % HALF, start % HALF + width)
            quantise(z_codes[start // HALF][:, places], z_scales[start // HALF][:, places], z_bf[n][:].rearrange("p s j -> p (s j)"))

        quantise_w2(0)
        nc.vector.tensor_copy(plane[0][:, S : 2 * S], plane[2][:])
        quantise_w2(1)
        for u in range(2):
            for n in range(2):
                round_pair(u, n, nc.vector.tensor_copy)
        round_pair(1, 2, nc.scalar.copy)
        quantise_z(0)
        quantise_z(1)
        upper = plane[0][:].rearrange("p (i s) -> p s i", i=2)
        for start in (0, P):
            nc.vector.tensor_copy(z_bf[2][:, start : start + P, 0:2], upper[:, HALF + start : HALF + start + P, :])
        for start in (0, P):
            places = slice(start, start + P)
            quantise(z_codes[1][:, places], z_scales[1][:, places], z_bf[2][:, places, :].rearrange("p s j -> p (s j)"))

        out_v = out.rearrange("(b p) s -> p b s", p=P)
        banks_in_turn = [n % BANKS for n in range(11, 0, -1)]

        def result(b, start, width, copy, staged):
            columns = slice(P * b, P * (b + 1))
            places = slice(start % HALF, start % HALF + width)
            acc = bank("out%d_%d" % (b, start), banks_in_turn.pop(), width)
            product(acc[:], w2_codes[:, columns], w2_scales[:, columns], z_codes[start // HALF][:, places], z_scales[start // HALF][:, places])
            copy(staged, acc[:])

        def stored(b, start, width, copy):
            staged = sbuf("staged%d_%d" % (b, start), [P, width], F32)
            result(b, start, width, copy, staged[:])
            nc.sync.dma_start(out_v[:, b, start : start + width], staged[:])

        stored(0, 0, P, nc.scalar.copy)
        stored(0, P, P, nc.scalar.copy)
        stored(1, 0, HALF, nc.scalar.copy)
        stored(2, 0, HALF, nc.scalar.copy)
        stored(3, 0, HALF, nc.vector.tensor_copy)
        staged_0 = sbuf("staged_0", [P, HALF], F32)
        result(0, HALF, P, nc.scalar.copy, staged_0[:, 0:P])
        result(0, HALF + P, P, nc.scalar.copy, staged_0[:, P:HALF])
        nc.sync.dma_start(out_v[:, 0, HALF:S], staged_0[:])
        stored(1, HALF, HALF, nc.vector.tensor_copy)
        stored(2, HALF, HALF, nc.scalar.copy)
        staged_last = sbuf("staged_last", [P, HALF], F32)
        result(3, HALF, P, nc.vector.tensor_copy, staged_last[:, 0:P])
        result(3, HALF + P, P, nc.vector.tensor_copy, staged_last[:, P:HALF])
        nc.sync.dma_start(out_v[:, 3, HALF:S], staged_last[:])
